import numpy as np, ml_dtypes
CORES = [6,15,38,47]
N = 4
BF = ml_dtypes.bfloat16
W, U, SH, B, T, DEL, LIM = 4096, 1024, 2, 256, 8, 4, 16
def parts(rng):
    return (rng.integers(0, 64, (N, 8, 16, W)), rng.integers(0, W, (N, 8, 16, U)), rng.integers(0, W, (N, 8, 16, B)), rng.integers(0, W, (N, 8, B)), rng.integers(0, 64, (N, 8, 16, B)))
def pack(x, canal, trail, cut, z):
    return {"x": x.reshape(N, 128, W).astype(np.float32).astype(BF), "canal": np.ascontiguousarray(canal.reshape(N, 128, U)).astype(np.int32), "trail": np.ascontiguousarray(trail.reshape(N, 128, B)).astype(np.int32),
            "cut": np.ascontiguousarray(cut).astype(np.int32), "z": z.reshape(N, 128, B).astype(np.float32).astype(BF)}
def setup_inputs(rng):
    return pack(*parts(rng))
def setup_inputs_spread(rng):
    def low(*shape): return np.minimum((W * rng.random(shape) ** 3).astype(np.int64), W - 1)
    def size(n): return np.minimum((64.0 ** rng.random((N, 8, 1, n)) * rng.random((N, 8, 16, n))).astype(np.int64), 63)
    return pack(size(W), low(N, 8, 16, U), low(N, 8, 16, B), low(N, 8, B), size(B))
def tips(rng, *shape):
    q = rng.random(shape)
    return np.where(q < 0.36, 0, np.where(q < 0.72, W - 1, rng.integers(0, W, shape)))
def setup_inputs_ends(rng):
    k = rng.random((N, 8, 1, W)); x = np.where(k < 0.2, 0, np.where(k < 0.4, 63, 63 * rng.integers(0, 2, (N, 8, 16, W))))
    one = (np.arange(16).reshape(1, 1, 16, 1) == rng.integers(0, 16, (N, 8, 1, W))) & (rng.random((N, 8, 1, W)) < 0.15)
    x = np.where(one, np.where(x == 63, 62, 1), x)
    for q in (1, N - 1): x[q] = np.where(rng.random((8, 1, W)) < 0.3, 32 + LIM + rng.integers(0, 3, (8, 1, W)), x[q])
    k = rng.random((N, 8, 1, B)); z = np.where(k < 0.3, 0, np.where(k < 0.45, 63, 63 * rng.integers(0, 2, (N, 8, 16, B))))
    for q in (0, 1, N - 1): z[q] = np.repeat(63 * rng.integers(0, 2, (8, 1, B)), 16, axis=1)
    z[:, :, :, B - 1] = 0
    canal, trail, cut = tips(rng, N, 8, 16, U), tips(rng, N, 8, 16, B), tips(rng, N, 8, B); cut[:, :, B - 1] = W - 1
    for r in range(N):
        for g in range(8):
            a = 2 * int(rng.integers(W // 8, W // 4)); b = a - 1; rows = rng.permutation(15)[:2]
            x[r, g, :, 0] = 0 if r in (0, 1, N - 1) else 63 * ((r + g) % 2)
            x[r, g, :, W - 1] = 63; x[r, g, :, a] = 63; x[r, g, :, b] = 63; x[r, g, int(rng.integers(0, 16)), b] = 62
            canal[r, g, :, U - 1] = W - 1; canal[r, g, rows[0], U - 1] = a; canal[r, g, rows[1], U - 1] = b
    w = 16 - DEL
    for q in (1, N - 1): trail[q, :, w] = np.where(z[q, :, 0] == 0, W - 1, 0)
    trail[1, 0, w, 0] = W - 1 - trail[1, 0, w, 0]
    trail[0, :, w] = np.where(z[0, :, 0] == 0, 0, W - 1)
    for q in range(2, N - 1):
        trail[q, 7, w] = np.where((trail[q, 7, w] >> SH) == U - 1, 0, trail[q, 7, w]); trail[q, 7, w, B - 1] = W - 1
    return pack(x, canal, trail, cut, z)
def setup_inputs_corners(rng):
    x, canal, trail, cut, z = parts(rng); s = int(rng.integers(0, 8)); H = 1 << SH
    for r in range(N):
        for g in range(8):
            kind = (r + g + s) % 8
            if kind == 0: cut[r, g] = (0, W - 1, int(rng.integers(0, W)))[r % 3]
            if kind == 1:
                u = rng.integers(0, U, (16, 1)); u[16 - DEL] = U - 1; u[17 - DEL if DEL > 1 else 0] = 0
                trail[r, g] = (u << SH) + rng.integers(0, H, (16, B))
            if kind == 2: trail[r, g] = (np.argsort(rng.random((16, U)), axis=1)[:, :B] << SH) + rng.integers(0, H, (16, B))
            if kind == 3:
                canal[r, g] = (np.arange(U)[None, :] << SH) + rng.integers(0, H, (16, U))
                cut[r, g] = rng.permutation(W)[:B]; trail[r, g] = cut[r, g][None, :]
            if kind == 4: x[r, g] = 30 + rng.integers(0, 4, (16, W)); z[r, g] = 30 + rng.integers(0, 4, (16, B))
            if kind == 5: x[r, g] = rng.integers(0, 4, (16, W)); z[r, g] = rng.integers(60, 64, (16, B))
            if kind == 6:
                at = np.argsort(rng.random((16, W)), axis=0); n = rng.integers(8, 10, (1, W)); sg = 2 * rng.integers(0, 2, (16, W)) - 1
                x[r, g] = 24 + sg * np.where(at < n, LIM + 1, LIM); z[r, g] = 24
            if kind == 7:
                x[r, g] = rng.integers(60, 64, (16, 4))[:, rng.integers(0, 4, W)]
                canal[r, g] = -np.sort(-canal[r, g], axis=0); canal[r, g, :, ::5] = canal[r, g, :1, ::5]
    return pack(x, canal, trail, cut, z)
def setup_inputs_full(rng):
    x, canal, trail, cut, z = parts(rng); w = 16 - DEL; w1 = (17 - DEL) % 16; H = 1 << SH; q = B // 4
    for r in range(N):
        for g in range(8):
            v = rng.integers(0, 64, W); y = np.full(B, 16); l = canal[r, g]; h = trail[r, g]
            if r == 0:
                h[w] = (rng.permutation(U)[:B] << SH) + rng.integers(0, H, B); v[h[w]] = rng.integers(40, 59, B)
            elif r == 1:
                o = rng.permutation(W - H); best = o[:B]; low = o[B:]
                v = rng.integers(0, 21, W); v[best] = rng.integers(25, 33, B)
                u = rng.permutation(U)[:B]; cut[r, g] = (u << SH) + rng.integers(0, H, B)
                l[:] = low[rng.integers(0, len(low), (16, U))]; l[rng.integers(0, 16, B), u] = best
                h[:] = rng.integers(0, W - H, (16, B))
                h[w, :B - 1] = (rng.permutation(U - 1)[:B - 1] << SH) + rng.integers(0, H, B - 1); h[w, B - 1] = W - 1
            elif r == 2:
                a = np.flatnonzero((v >= 16) & (v <= 32)); h[w] = a[rng.integers(0, len(a), B)]; h[w1] = a[rng.integers(0, len(a), B)]
                if g in (0, 3, 7):
                    far = np.flatnonzero(v >= 40); i = 0 if g == 0 else B - 1 if g == 7 else int(rng.integers(0, B))
                    h[w, i] = far[int(rng.integers(0, len(far)))]
            else:
                v = rng.integers(0, 63, W); v[0] = 63; v[W - 1] = 63
                y = rng.integers(0, 64, B); i = rng.permutation(B); u = rng.permutation(U - 1)[:2 * q]
                y[i[:q]] = 63; y[i[q:2 * q]] = 0; cut[r, g, i[:2 * q]] = (u << SH) + rng.integers(0, H, 2 * q)
                l[:, u[:q]] = W - 1; l[:, u[q:]] = rng.integers(1, W - 1, (16, q))
                l[rng.integers(0, 2, q), u[q:]] = 0; l[rng.integers(13, 16, q), u[q:]] = W - 1
            x[r, g] = v; z[r, g] = y
            if r > 2: x[r, g, int(rng.integers(0, 16)), 0] = 62
    return pack(x, canal, trail, cut, z)
def setup_inputs_meet(rng):
    x, canal, trail, cut, z = parts(rng)
    for r in range(N):
        for g in range(8):
            s = rng.permutation(W)[:64]; s[0] = W - 1
            canal[r, g] = s[rng.integers(0, 64, (16, U))]; trail[r, g] = s[rng.integers(0, 64, (16, B))]; cut[r, g] = s[rng.integers(0, 64, B)]
    return pack(x, canal, trail, cut, z)
def check_inputs(d):
    bad = []
    for k, hi in (("x", 63), ("canal", W - 1), ("trail", W - 1), ("cut", W - 1), ("z", 63)):
        a = np.asarray(d[k]).astype(np.float64)
        if not (np.min(a) >= 0 and np.max(a) <= hi): bad.append("range of " + k)
        if not np.all(a == np.floor(a)): bad.append("whole numbers in " + k)
    return bad
def reference(x, canal, trail, cut, z):
    X = x.astype(np.float32).astype(np.int64).reshape(N, 8, 16, W); C = canal.astype(np.int64).reshape(N, 8, 16, U); G = trail.astype(np.int64).reshape(N, 8, 16, B)
    V = cut.astype(np.int64).reshape(N, 8, B); Z = z.astype(np.float32).astype(np.int64).reshape(N, 8, 16, B); skips = np.zeros(N, np.int64)
    for t in range(T):
        lim = LIM + (skips & 3); skips = np.zeros(N, np.int64); come = np.zeros_like(Z); row = (t + 16 - DEL) % 16
        for r in range(N):
            for g in range(8):
                a, l, h, q = X[r, g], C[r, g], G[r, g], Z[r, g]
                k = l[:, V[r, g] >> SH]
                score = np.add.reduce(np.maximum(a[:, k] - q[:, None, :], 0), axis=0)
                c = np.min(np.where(score == np.max(score, axis=0), k, W), axis=0)
                cut_off = np.sum(np.abs(a[:, h] - q[:, None, :]) > lim[r], axis=0) >= 9
                w = h[row] + 0; skip = cut_off[row]; xw = a[:, w]; xc = a[:, c]
                first = np.zeros(B, bool); first[np.unique(w >> SH, return_index=True)[1]] = True
                new = np.where(skip, np.minimum(xw + 4, 63), (xw + q) >> 1)
                a[:, w[first]] = new[:, first]
                m = first & ~skip; u = w[m] >> SH
                l[:, u] = np.where(cut_off[:, m], l[:, u], h[:, m])
                h[:] = np.where(cut_off, k, h); h[t] = c
                a[:, c] = xc >> 1
                V[r, g] = c; skips[r] += np.sum(skip)
                come[(r + 1 + t % (N - 1)) % N, g] = (q + xc) >> 1
        Z = come
    return {"yx": X.reshape(N, 128, W).astype(np.float32).astype(BF), "yl": C.reshape(N, 128, U).astype(np.float32), "yg": G.reshape(N, 128, B).astype(np.float32)}

@@ -1,0 +1,489 @@
+from concourse.mybir import AluOpType, AxisListType, ActivationFunctionType
+
+A = AluOpType
+AF = ActivationFunctionType
+NT = 8
+BIAS = 160.0
+XW = 5136
+CW = 1296
+
+F4, BF, HF, I4, U2 = "float32", "bfloat16", "float16", "int32", "uint16"
+SCRATCH = {}
+for _n, _s, _d in (
+        ("X", XW, BF), ("CAN", CW, F4), ("cin", 1024, I4), ("tin", 256, I4), ("vin", 256, I4),
+        ("xg0", 4096, BF), ("xg1", 4096, BF), ("ab", 4096, BF), ("th", 4096, BF), ("zrep", 4096, BF), ("sc", 4096, BF),
+        ("lo", 1024, F4), ("go", 256, F4), ("eqw", 3072, BF), ("eqc", 3072, BF), ("wrow", 2048, HF), ("wall", 2048, HF),
+        ("sco", 256, F4), ("q1", 16, I4), ("q2", 16, I4), ("UW", 256, HF), ("SPs", 256, HF), ("LwU", 32, F4),
+        ("nw", 16, F4), ("n1w", 16, F4), ("nc", 16, F4), ("n1c", 16, F4), ("A1", 256, HF), ("A2c", 256, HF), ("A2w", 256, HF),
+        ("dwi", 16, I4), ("dws", 16, I4), ("uf", 16, HF), ("xs", 256, HF), ("xw", 256, BF), ("r2", 256, BF), ("r2m", 256, BF),
+        ("rn", 256, BF), ("cw", 256, F4), ("cm", 256, F4), ("cn", 256, F4), ("gm", 256, HF), ("sevL", 256, BF), ("sevT", 256, BF),
+        ("skrep", 256, BF), ("sf", 1, F4), ("si", 1, I4), ("s3", 1, I4), ("lim", 8, F4),
+        ("Z", 256 * NT, BF), ("ZS", 256 * NT, BF),
+        ("i128", 128, F4), ("pc", 1, F4), ("pci", 1, I4), ("pg", 1, F4), ("pk", 1, F4), ("p16", 1, F4),
+        ("rc", 1, F4), ("k272", 272, F4), ("w144", 144, F4), ("v1", 256, F4), ("zli", 256, I4),
+        ("skli", 128, I4), ("zl", 256, U2), ("skl", 128, U2), ("RM", 16, F4), ("RM1", 16, F4), ("RM2", 16, F4), ("RMn", 16, F4),
+        ("I16", 128, HF), ("I8n", 128, BF), ("I8p", 128, BF), ("Ib", 128, BF), ("Ibn", 128, BF), ("Ih", 128, BF), ("I5n", 128, BF),
+        ("It", 1024, HF), ("blkf", 8, F4), ("blk1", 8, HF), ("blkb", 8, BF), ("blkS", 8, BF), ("onesg", 1024, HF), ("ones16", 256, HF),
+        ("onesb", 128, BF), ("qtr", 128, HF), ("dmask", 256, HF), ("in1c", 256, HF), ("selk", 64, HF), ("wide", 144, HF),
+        ("thrk", 272, F4), ("resetv", 256, F4), ("wtf", 1, F4), ("wt", 1, BF), ("wbig", 1, BF), ("thr", 1, F4)):
+    SCRATCH[_n] = ("sbuf", [128, _s], _d)
+for _k in range(2):
+    for _n, _s, _d in (("Kn", 256, HF), ("Ku", 256, U2), ("Gn", 256, HF), ("Gu", 256, U2), ("cutv", 256, BF), ("Lc", 16, F4),
+                       ("cu", 16, U2), ("vl", 16, U2), ("dwu", 16, U2), ("dwl", 16, U2), ("dcu", 16, U2)):
+        SCRATCH["%s%d" % (_n, _k)] = ("sbuf", [128, _s], _d)
+for _k in range(8):
+    SCRATCH["ps%d" % _k] = ("psum", [128, 512], F4)
+
+SEMAPHORES = (["qv", "qs", "qt", "qg"] + ["ld_" + n for n in ("cut", "z", "trail", "canal", "x0", "x1", "x2", "x3")]
+              + ["st_" + n for n in ("o0", "o1", "o2", "o3", "ol", "og")] + ["row%d" % k for k in range(NT)]
+              + ["arr%d" % k for k in range(1, NT)] + ["snt%d" % k for k in range(1, NT)])
+
+CY, GA, PEC, SYNC = 0.00083, 1.5, 0.0006, 0.1
+
+
+def dv(n): return 0.06 + n * CY
+def dh(n): return 0.06 + max(n * 0.5, 64) * CY
+def dg(n): return 0.05 + n * GA * CY
+def ds(n): return 0.05 + n * 3.5 * CY
+def sg(n): return 0.065 + n * GA * CY
+def sa(n): return 0.065 + n * CY
+def pe(*ns): return sum(max(64, n) for n in ns) * PEC + 0.02
+
+
+def rank_program(g, core, T, topo):
+    rank = T.rank_of(core)
+    if rank is None:
+        return
+    V, S, PE, Y = g.vector, g.scalar, g.tensor, g.sync
+    ops = []
+
+    def op(eng, cost, calls, R=(), W=(), tile=None, lat=0.0, sem=None, cnt=0):
+        ops.append({"e": eng, "c": cost, "f": calls, "R": list(R), "W": list(W), "tile": tile, "lat": lat,
+                    "sem": sem, "cnt": cnt, "i": len(ops)})
+
+    def v(cost, f, R, W): op("v", cost, [f], R, W)
+    def s(cost, f, R, W): op("s", cost, [f], R, W)
+    def vp(cost, f, tile, R, W): op("v", cost, lambda B: [lambda: f(B)], R, W, tile=tile)
+    mm = PE.matmul
+
+    def ts(out, i0, s1, s2, o0, o1=None):
+        if o1 is None:
+            return V.tensor_scalar(out, i0, s1, None, o0)
+        return V.tensor_scalar(out, i0, s1, s2, o0, o1)
+
+    def load(name, out, src, W, lat, R=()):
+        op("y", 0.1, [lambda: Y.dma_start(out, src)], R, W, lat=lat, sem="ld_" + name, cnt=16)
+
+    v(dv(256), lambda: V.memset(T.vin[:], 0), [], ["vin"])
+    v(dv(512), lambda: V.memset(T.X[:, 4096:XW], BIAS), [], ["Xd"])
+    v(dv(272), lambda: V.memset(T.CAN[:, 1024:CW], 0.0), [], ["CANd"])
+    load("z", T.xw[:], T.z[:], ["xw"], 2.0)
+    load("trail", T.tin[:], T.trail[:], ["tin"], 2.2)
+    load("canal", T.cin[:], T.canal[:], ["cin"], 4.0)
+    for q in range(4):
+        load("x%d" % q, T.X[:, 1024 * q:1024 * q + 1024], T.x[:, 1024 * q:1024 * q + 1024], ["X%d" % q], 4.0 + q)
+    load("cut", T.vin[0:128:16, :], T.cut[:], ["vin2"], 2.0, ["vin"])
+    XC = ["X0", "X1", "X2", "X3"]
+    XR = XC + ["Xd"]
+
+    def iota(name, out, pat, base, cm, f=True):
+        n = 1
+        for a, b in pat:
+            n *= b
+        kw = {"allow_small_or_imprecise_dtypes": True} if f else {}
+        op("g", 0.13 + 2 * n * CY, [lambda: g.iota(out, pat, base, cm, **kw)], [], [name])
+
+    iota("pci", T.pci[:], [[0, 1]], 0, 1, False)
+    iota("pc", T.pc[:], [[0, 1]], 0, 1)
+    iota("i128", T.i128[:], [[1, 128]], 0, 0)
+    iota("k272", T.k272[:], [[0, 17], [1, 16]], 0, 0)
+    iota("zli", T.zli[:], [[1, 256]], 0, 0, False)
+    iota("v1", T.v1[:], [[-512, 2], [0, 128]], -2052, -4)
+    iota("w144", T.w144[:], [[1, 144]], -15, 0)
+    iota("sklia", T.skli[:, 0:64], [[1, 4], [16, 16]], 12, 0, False)
+    iota("sklib", T.skli[:, 64:128], [[1, 4], [16, 16]], 0, 0, False)
+    one = dv(64)
+    v(one, lambda: ts(T.q1[:, 0:1], T.pci[:], 4, None, A.arith_shift_right), ["pci"], ["q1"])
+    v(one, lambda: ts(T.q2[:, 0:1], T.pci[:], 15, None, A.bitwise_and), ["pci"], ["q2"])
+    v(one, lambda: V.tensor_copy(T.pg[:], T.q1[:, 0:1]), ["q1"], ["pg"])
+    v(one, lambda: V.tensor_copy(T.pk[:], T.q2[:, 0:1]), ["q2"], ["pk"])
+    v(one, lambda: ts(T.p16[:], T.pg[:], 16.0, None, A.mult), ["pg"], ["p16"])
+    v(one, lambda: ts(T.rc[:], T.pk[:], 0.0, 2048.0, A.is_equal, A.mult), ["pk"], ["rc"])
+    v(one, lambda: ts(T.RM[:], T.i128[:, 0:16], T.pk[:], None, A.is_equal), ["i128", "pk"], ["RM"])
+    v(one, lambda: ts(T.RM1[:], T.RM[:], 0.25, None, A.mult), ["RM"], ["RM1"])
+    v(one, lambda: ts(T.RM2[:], T.RM[:], 1536.375, None, A.mult), ["RM"], ["RM2"])
+    v(one, lambda: ts(T.RMn[:], T.RM[:], -1.0, 1.0, A.mult, A.add), ["RM"], ["RMn"])
+    for name, val in (("I16", 1.0), ("Ib", 1.0), ("Ibn", -1.0), ("I8n", -8192.0), ("I8p", 8192.0), ("Ih", 0.5), ("I5n", -512.0)):
+        v(dv(128), lambda name=name, val=val: ts(T[name][:], T.i128[:], T.pc[:], val, A.is_equal, A.mult), ["i128", "pc"], [name])
+    for name, val in (("blkf", 1.0), ("blk1", 1.0), ("blkb", 1.0), ("blkS", 4096.0)):
+        v(one, lambda name=name, val=val: ts(T[name][:], T.i128[:, 0:8], T.pg[:], val, A.is_equal, A.mult), ["i128", "pg"], [name])
+    v(dh(256), lambda: V.tensor_scalar(T.ones16[:], T.k272[:, 0:256], 0.0, 1.0, A.mult, A.add), ["k272"], ["ones16"])
+    v(dh(128), lambda: V.memset(T.onesb[:], 1.0), [], ["onesb"])
+    v(dh(128), lambda: ts(T.qtr[:], T.ones16[:, 0:128], -0.25 / 128, None, A.mult), ["ones16"], ["qtr"])
+    v(one, lambda: V.memset(T.wbig[:], float(2.0 ** 90)), [], ["wbig"])
+    v(one, lambda: V.memset(T.lim[:, 0:1], 16.0), [], ["lim0"])
+    op("v", 8 * dh(128), [lambda k=k: ts(T.onesg[:, 128 * k:128 * k + 128], T.ones16[:, 0:128], T.blkf[:, k:k + 1], None, A.mult)
+                          for k in range(8)], ["ones16", "blkf"], ["onesg"])
+    v(dv(256), lambda: ts(T.dmask[:], T.k272[:, 0:256], T.pk[:], None, A.is_equal), ["k272", "pk"], ["dmask"])
+    v(dv(256), lambda: ts(T.resetv[:], T.k272[:, 0:256], 0.0, -2.0e7, A.is_equal, A.mult), ["k272"], ["resetv"])
+    v(dv(272), lambda: ts(T.sco[:], T.v1[:], -4096.0, None, A.add), ["v1"], ["sco"])
+    v(dv(512), lambda: V.tensor_tensor(T.go[:], T.sco[:], T.dmask[:], A.mult), ["sco", "dmask"], ["go"])
+    v(dv(256), lambda: ts(T.in1c[:], T.go[:], 4096.0, None, A.add), ["go"], ["in1c"])
+    v(dv(272), lambda: ts(T.thrk[:], T.k272[:], 15.0, 100.0, A.is_equal, A.mult), ["k272"], ["thrk0"])
+    v(dv(272), lambda: ts(T.thrk[:], T.thrk[:], 8.5, None, A.add), ["thrk0"], ["thrk"])
+    v(dv(144), lambda: ts(T.wide[:], T.w144[:], T.p16[:], None, A.is_equal), ["w144", "p16"], ["wide"])
+    v(dv(256), lambda: V.tensor_copy(T.zl[:], T.zli[:]), ["zli"], ["zl"])
+    v(dv(128), lambda: V.tensor_copy(T.skl[:], T.skli[:]), ["sklia", "sklib"], ["skl"])
+    op("v", 8 * one, [lambda t=t: ts(T.selk[:, 8 * t:8 * t + 8], T.blkf[:], T.RM[:, (t + 12) % 16:(t + 12) % 16 + 1], None, A.mult)
+                      for t in range(NT)], ["blkf", "RM"], ["selk"])
+    op("v", 8 * dh(128), [lambda t=t: ts(T.It[:, 128 * t:128 * t + 128], T.I16[:], T.RMn[:, t:t + 1], None, A.mult)
+                          for t in range(NT)], ["I16", "RMn"], ["It"])
+    v(dv(128), lambda: V.memset(T.cm[:, 0:128], 0.5), [], ["cm"])
+    v(dv(128), lambda: V.memset(T.cn[:, 0:128], 0.0), [], ["cn"])
+    v(dv(128), lambda: V.tensor_tensor_scan(T.cw[:, 0:128], T.cm[:, 0:128], T.cn[:, 0:128], float(2.0 ** 64), A.mult, A.add), ["cm", "cn"], ["cw"])
+    v(dv(256), lambda: V.tensor_tensor(T.lo[:, 0:128], T.cw[:, 0:128], T.I16[:], A.mult), ["cw", "I16"], ["lo"])
+    v(dv(128), lambda: V.tensor_reduce(T.wtf[:], T.lo[:, 0:128], AxisListType.X, A.add), ["lo"], ["wtf"])
+    v(one, lambda: V.tensor_copy(T.wt[:], T.wtf[:]), ["wtf"], ["wt"])
+    v(one, lambda: ts(T.thr[:], T.wtf[:], 2.5, None, A.mult), ["wtf"], ["thr"])
+
+    v(dv(256), lambda: ts(T.UW[:], T.vin[:], -1.0, T.rc[:], A.mult, A.add), ["vin", "vin2", "rc"], ["UW"])
+    v(dv(256), lambda: ts(T.Gn0[:], T.tin[:], -1.0, 2048.0, A.mult, A.add), ["tin"], ["Gn0"])
+    v(dv(256), lambda: V.tensor_copy(T.Gu0[:], T.tin[:]), ["tin"], ["Gu0"])
+    v(dh(256), lambda: ts(T.Z[:, 0:256], T.xw[:], BIAS, None, A.add), ["xw"], ["Z0"])
+    v(dv(1024), lambda: ts(T.CAN[:, 0:1024], T.cin[:], -1.0, 2048.0, A.mult, A.add), ["cin"], ["CAN"])
+    for q in range(4):
+        v(dh(1024), lambda q=q: ts(T.X[:, 1024 * q:1024 * q + 1024], T.X[:, 1024 * q:1024 * q + 1024], BIAS, None, A.add),
+          ["X%d" % q], ["X%d" % q])
+
+    def halves(src, rhs):
+        return lambda B: [lambda h=h: mm(B[:, 8 * h:8 * h + 8], T[src][:, 128 * h:128 * h + 128], rhs, True, True) for h in range(2)]
+
+    def spread_lists(key, tname):
+        op("t", pe(64, 64), halves(key, T.blk1[:]), [key, "blk1"], [], tile=tname)
+
+    def same(t, tag, src, col0, Lname, eq, pb):
+        k0 = (t + 12) % 16
+        if pb:
+            op("y", 0.1, [lambda: Y.dma_start(T.wrow[0:1, :], T[src][k0:128:16, :])], [src], ["wrow"], lat=2.0, sem="row%d" % t, cnt=16)
+            op("g", 0.14 + 4 * 2048 * CY, [lambda: g.partition_broadcast(T.wall[:], T.wrow[0:1, :], 128)], ["wrow"], ["wall"])
+        for b in range(4):
+            ks = (2 * b, 2 * b + 1)
+
+            def cmp(W, off, k, h):
+                return lambda: ts(T[eq][:, 384 * k + 256 * h:384 * k + 256 + 128 * h], W[:, off + 128 * h:off + 256],
+                                  T[Lname][:, col0 + 8 * h + k:col0 + 8 * h + k + 1], None, A.is_equal)
+            if pb:
+                op("v", 2 * dh(256) + 2 * dh(128), [cmp(T.wall, 256 * k, k, h) for k in ks for h in range(2)], [Lname, "wall"], ["%s_%d" % (eq, b)])
+            else:
+                tn = "BC%s%d_%d" % (tag, t, b)
+                op("t", pe(256, 256), lambda B, ks=ks: [lambda k=k: mm(B[:, 256 * (k % 2):256 * (k % 2) + 256], T.onesg[:, 128 * k:128 * k + 128],
+                   T[src][:], True, True) for k in ks], [src, "onesg"], [], tile=tn)
+                op("v", 2 * dv(256) + 2 * dv(128), lambda B, ks=ks, cmp=cmp: [cmp(B, 256 * (k % 2), k, h) for k in ks for h in range(2)],
+                   [Lname], ["%s_%d" % (eq, b)], tile=tn)
+        tn = "EQ%s%d" % (tag, t)
+        for b in range(4):
+            def sums(B, b=b):
+                r = []
+                for k in (2 * b, 2 * b + 1):
+                    o = 384 * k
+                    r.append(lambda k=k, o=o: mm(B[:, k:k + 1], T[eq][:, o:o + 128], T.wt[:], True, True))
+                    r.append(lambda k=k, o=o: mm(B[:, 8 + k:9 + k], T[eq][:, o + 128:o + 256], T.wbig[:], True, False))
+                    r.append(lambda k=k, o=o: mm(B[:, 8 + k:9 + k], T[eq][:, o + 256:o + 384], T.wt[:], False, True))
+                return r
+            op("t", pe(64, 64, 64, 64, 64, 64), sums, ["%s_%d" % (eq, b), "wt", "wbig"], [], tile=tn)
+        return tn
+
+    def place(t, par, first):
+        v(dg(256), lambda: V.tensor_tensor(T.A1[:], T["Lc%d" % par][:, 0:16].indirect(T.zl[:, 0:16]), T.dmask[:], A.mult),
+          ["Lc%d" % par, "zl", "dmask"], ["A1"])
+        tn = "cW%d" % t
+        spread_lists("A1", tn)
+        if not first:
+            vp(one, lambda B: ts(T["cu%d" % par][:], B[:, 0:16], -1.0, 2048.0, A.mult, A.add), tn, [], ["cu%d" % par])
+        if t < NT - 1:
+            vp(one, lambda B: ts(T.uf[:], B[:, 0:16], 0.25, 1536.375, A.mult, A.add), tn, [], ["uf"])
+            v(one, lambda: ts(T["vl%d" % par][:], T.uf[:], -1.0, 2048.0, A.mult, A.add), ["uf"], ["vl%d" % par])
+
+    op("t", pe(64, 64), halves("UW", T.blk1[:]), ["UW", "blk1"], [], tile="cut0")
+    vp(one, lambda B: V.tensor_copy(T.Lc1[:], B[:, 0:16]), "cut0", [], ["Lc1"])
+    place(-1, 1, True)
+
+    def step(t):
+        p, q = t % 2, 1 - t % 2
+        last = t == NT - 1
+        k0 = (t + 12) % 16
+        Z, Kn, Ku, Gn, Gu, xg = "Z%d" % t, "Kn%d" % p, "Ku%d" % p, "Gn%d" % p, "Gu%d" % p, "xg%d" % p
+        Lc, cu, dcu, dwu, dwl, cutv = "Lc%d" % p, "cu%d" % p, "dcu%d" % p, "dwu%d" % p, "dwl%d" % p, "cutv%d" % p
+        Gn1, Gu1, vl = "Gn%d" % q, "Gu%d" % q, "vl%d" % q
+        z0, z1 = 256 * t, 256 * t + 256
+        v(dg(256), lambda: V.tensor_copy(T[Kn][:], T.CAN[:, 0:1024].indirect(T[vl][:])), ["CAN", vl], [Kn])
+        v(dh(256), lambda: ts(T[Ku][:], T[Kn][:], -1.0, 2048.0, A.mult, A.add), [Kn], [Ku])
+        for c in range(4):
+            s(sg(1024), lambda c=c: S.activation(T[xg][:, 1024 * c:1024 * c + 1024],
+              T.X[:, 0:4096].indirect(T[Gu][:, 64 * c:64 * c + 64]), AF.Copy), XC + [Gu], ["%s_%d" % (xg, c)])
+        v(dh(256), lambda: ts(T.UW[:], T[Gn][:], T.RM1[:, k0:k0 + 1], T.RM2[:, k0:k0 + 1], A.mult, A.add), [Gn, "RM1", "RM2"], ["UW"])
+
+        def callsL(B):
+            r = []
+            for h in range(2):
+                r.append(lambda h=h: mm(B[:, 8 * h:8 * h + 8], T[Gn][:, 128 * h:128 * h + 128], T.selk[:, 8 * t:8 * t + 8], True, True))
+                r.append(lambda h=h: mm(B[:, 16 + 8 * h:24 + 8 * h], T.UW[:, 128 * h:128 * h + 128], T.blk1[:], True, True))
+            return r
+        op("t", pe(64, 64, 64, 64), callsL, [Gn, "UW", "selk", "blk1"], [], tile="LwU%d" % t)
+        op("s", sa(32), lambda B: [lambda: S.activation(T.LwU[:], B[:, 0:32], AF.Copy)], [], ["LwU"], tile="LwU%d" % t)
+        tn = same(t, "w", "UW", 16, "LwU", "eqw", True)
+        vp(one, lambda B: ts(T.nw[:], B[:, 0:16], T.thr[:], -10000.0, A.is_gt, A.mult), tn, ["thr"], ["nw"])
+        v(one, lambda: V.tensor_tensor(T.n1w[:], T.nw[:], T.LwU[:, 0:16], A.add), ["nw", "LwU"], ["n1w"])
+        v(dg(256), lambda: V.tensor_tensor(T.A2w[:], T.n1w[:, 0:16].indirect(T.zl[:, 0:16]), T.in1c[:], A.max), ["n1w", "zl", "in1c"], ["A2w"])
+        spread_lists("A2w", "W2w%d" % t)
+        vp(one, lambda B: ts(T.dwi[:], B[:, 0:16], -1.0, 63488.0, A.mult, A.add), "W2w%d" % t, [], ["dwi"])
+        v(one, lambda: V.tensor_copy(T[dwu][:], T.dwi[:]), ["dwi"], [dwu])
+        v(one, lambda: ts(T.dws[:], T.dwi[:], 2, None, A.arith_shift_right), ["dwi"], ["dws"])
+        v(one, lambda: V.tensor_copy(T[dwl][:], T.dws[:]), ["dws"], [dwl])
+        s(sg(256), lambda: S.activation(T.xw[:], T.X[:].indirect(T[dwu][:]), AF.Copy), XR + [dwu], ["xw"])
+        s(sg(256), lambda: S.activation(T.cw[:], T.CAN[:].indirect(T[dwl][:]), AF.Copy), ["CAN", "CANd", dwl], ["cw"])
+        v(dh(256), lambda: ts(T.r2[:], T.xw[:], 4.0, BIAS + 63.0, A.add, A.min), ["xw"], ["r2"])
+        for h in range(2):
+            s(sg(2048), lambda h=h: S.activation(T.zrep[:, 2048 * h:2048 * h + 2048], T.Z[:, z0:z1].indirect(T.zl[:, 128 * h:128 * h + 128]), AF.Copy),
+              [Z, "zl"], ["zrep%d" % h])
+        for h in range(2):
+            v(dg(2048), lambda h=h: V.tensor_tensor(T.sc[:, 2048 * h:2048 * h + 2048], T.X[:, 0:4096].indirect(T[Ku][:, 128 * h:128 * h + 128]),
+              T.zrep[:, 2048 * h:2048 * h + 2048], A.max), XC + [Ku, "zrep%d" % h], ["sc%d" % h])
+
+            def callsK(B, h=h):
+                r = [lambda: mm(B[:, 128 * h:128 * h + 128], T[Kn][:, 128 * h:128 * h + 128], T.I16[:], True, False)]
+                for k in range(16):
+                    r.append(lambda k=k: mm(B[:, 128 * h + k:128 * h + 128:16], T.sc[:, 2048 * h + k:2048 * h + 2048:16], T.blkS[:], False, k == 15))
+                return r
+            op("t", pe(128, *([64] * 16)), callsK, [Kn, "I16", "blkS", "sc%d" % h], [], tile="key%d" % t)
+        vp(dv(256), lambda B: V.tensor_tensor_scan(T.sco[:], T.resetv[:], B[:, 0:256], 0.0, A.add, A.max), "key%d" % t, ["resetv"], ["sco"])
+        v(one, lambda: ts(T.q1[:], T.sco[:, 15:256:16], 2047.0, None, A.add), ["sco"], ["q1"])
+        v(one, lambda: ts(T.q2[:], T.q1[:], 4095, None, A.bitwise_and), ["q1"], ["q2"])
+        v(one, lambda: ts(T[Lc][:], T.q2[:], -2047.0, None, A.add), ["q2"], [Lc])
+        place(t, p, False)
+        if not last:
+            snt, arr = "snt%d" % (t + 1), "arr%d" % (t + 1)
+            v(dg(256), lambda: V.tensor_tensor(T.xs[:], T.X[:, 0:4096].indirect(T[cu][:]), T.Z[:, z0:z1], A.add), XC + [cu, Z], ["xs"])
+            v(dh(256), lambda: ts(T.ZS[:, z0:z1], T.xs[:], 0.5, -0.25, A.mult, A.add), ["xs"], ["zs%d" % t])
+            dst = T.cores[(rank + 1 + t % 3) % len(T.cores)]
+            rid, pid = topo.addr(dst)[0], topo.addr(dst)[1]
+            ne = len(topo.engines(core, dst))
+            op("g", 1.0, [lambda: g.remote_dma(T.Z[:, z1:z1 + 256], T.ZS[:, z0:z1], T.sem[arr], T.sem[snt], pid=pid, routing_id=rid,
+                                               dma_engine_mask=topo.mask(core, dst))], ["zs%d" % t], ["way%d" % t], sem=snt, cnt=ne)
+            op("x", 0.0, [], ["way%d" % t], ["Z%d" % (t + 1)], lat=2.5, sem=arr, cnt=ne)
+        s(sg(256), lambda: S.activation(T[cutv][:], T.X[:, 0:4096].indirect(T[cu][:]), AF.Identity, bias=BIAS / 2 - 0.25, scale=0.5), XC + [cu], [cutv])
+        op("t", pe(128, 128), lambda B: [lambda h=h: mm(B[:, 128 * h:128 * h + 128], T.A1[:, 128 * h:128 * h + 128], T.I16[:], True, True)
+                                         for h in range(2)], ["A1", "I16"], [], tile="SP%d" % t)
+        vp(dv(256), lambda B: V.tensor_copy(T.SPs[:], B[:, 0:256]), "SP%d" % t, [], ["SPs"])
+        tn = same(t, "c", "SPs", 0, Lc, "eqc", False)
+        vp(one, lambda B: ts(T.nc[:], B[:, 0:16], T.thr[:], -10000.0, A.is_gt, A.mult), tn, ["thr"], ["nc"])
+        v(one, lambda: V.tensor_tensor(T.n1c[:], T.nc[:], T[Lc][:], A.add), ["nc", Lc], ["n1c"])
+        v(dg(256), lambda: V.tensor_tensor(T.A2c[:], T.n1c[:, 0:16].indirect(T.zl[:, 0:16]), T.in1c[:], A.max), ["n1c", "zl", "in1c"], ["A2c"])
+        spread_lists("A2c", "W2c%d" % t)
+        vp(one, lambda B: ts(T[dcu][:], B[:, 0:16], -1.0, 63488.0, A.mult, A.add), "W2c%d" % t, [], [dcu])
+        for b in range(8):
+            tn = "d%d_%d" % (t, b)
+
+            def callsD(B, b=b):
+                r = []
+                for j in range(2):
+                    r.append(lambda j=j: mm(B[:, 256 * j:256 * j + 256], T.Ib[:], T[xg][:, 2 * b + j:4096:16], True, False))
+                    r.append(lambda j=j: mm(B[:, 256 * j:256 * j + 256], T.Ibn[:], T.Z[:, z0:z1], False, True))
+                return r
+            op("t", pe(256, 256, 256, 256), callsD, ["Ib", "Ibn", Z] + ["%s_%d" % (xg, c) for c in range(4)], [], tile=tn)
+            op("s", sa(512), lambda B, b=b: [lambda: S.activation(T.ab[:, 512 * b:512 * b + 512], B[:], AF.Abs)], [], ["ab%d" % b], tile=tn)
+            if b % 2 == 1:
+                c = b // 2
+                v(dh(1024), lambda c=c: ts(T.th[:, 1024 * c:1024 * c + 1024], T.ab[:, 1024 * c:1024 * c + 1024], T.lim[:, t:t + 1], None, A.is_gt),
+                  ["ab%d" % (b - 1), "ab%d" % b, "lim%d" % t], ["th%d" % c])
+        for c in range(4):
+            op("t", pe(*([64] * 8)), lambda B, c=c: [
+                lambda k=k, h=h: mm(B[:, 128 * h + k:128 * h + 128:16], T.th[:, 256 * k + 128 * h:256 * k + 128 * h + 128], T.blkb[:], True, True)
+                for k in range(4 * c, 4 * c + 4) for h in range(2)], ["th%d" % c, "blkb"], [], tile="cnt%d" % t)
+        vp(dv(256), lambda B: ts(T.sevL[:], B[:, 0:256], 8.5, None, A.is_gt), "cnt%d" % t, [], ["sevL"])
+        vp(dv(256), lambda B: V.tensor_tensor(T.sevT[:], B[:, 0:256], T.thrk[:, 15 - t:271 - t], A.is_gt), "cnt%d" % t, ["thrk"], ["sevT"])
+        s(sg(256), lambda: S.activation(T.skrep[:], T.sevL[:].indirect(T.skl[:, 16 * t:16 * t + 16]), AF.Copy), ["sevL", "skl"], ["skrep"])
+        if not last:
+            op("t", pe(64), lambda B: [lambda: mm(B[:, 0:16], T.onesb[:], T.sevL[:, k0:256:16], True, True)], ["onesb", "sevL"], [], tile="S%d" % t)
+            vp(one, lambda B: V.tensor_reduce(T.sf[:], B[:, 0:16], AxisListType.X, A.add), "S%d" % t, [], ["sf"])
+            v(one, lambda: V.tensor_copy(T.si[:], T.sf[:]), ["sf"], ["si"])
+            v(one, lambda: ts(T.s3[:], T.si[:], 3, None, A.bitwise_and), ["si"], ["s3"])
+            v(one, lambda: ts(T.lim[:, t + 1:t + 2], T.s3[:], 16.0, None, A.add), ["s3"], ["lim%d" % (t + 1)])
+
+        def blend(ident, extra, sevs):
+            def calls(B):
+                r = []
+                for o, m in ((0, "I8n"), (256, "I8p")):
+                    r.append(lambda o=o: mm(B[:, o:o + 256], ident, T[Gn][:], True, False))
+                    if extra:
+                        r.append(lambda o=o: mm(B[:, o:o + 256], T.wide[:, 15 - t:143 - t], T.SPs[:], False, False))
+                    for n in sevs:
+                        for h in range(2):
+                            r.append(lambda o=o, m=m, h=h, n=n: mm(B[:, o + 128 * h:o + 128 * h + 128], T[n][:, 128 * h:128 * h + 128], T[m][:],
+                                                                   False, h == 1 and n == sevs[-1]))
+                return r
+            return calls
+        op("t", pe(*([256] * 6)), blend(T.It[:, 128 * t:128 * t + 128], True, ["sevT"]),
+           ["It", Gn, "wide", "SPs", "sevT", "I8n", "I8p"], [], tile="G%d" % t)
+        vp(dv(256), lambda B: V.tensor_tensor(T.gm[:], T[Kn][:], B[:, 0:256], A.max), "G%d" % t, [Kn], ["gm"])
+        vp(dv(256), lambda B: V.tensor_tensor(T[Gn1][:], T.gm[:], B[:, 256:512], A.min), "G%d" % t, ["gm"], [Gn1])
+        if not last:
+            v(dh(256), lambda: ts(T[Gu1][:], T[Gn1][:], -1.0, 2048.0, A.mult, A.add), [Gn1], [Gu1])
+        op("t", pe(*([256] * 6)), blend(T.I16[:], False, ["sevL", "skrep"]), ["I16", Gn, "sevL", "skrep", "I8n", "I8p"], [], tile="N%d" % t)
+        vp(dv(256), lambda B: V.tensor_tensor(T.cm[:], T.cw[:], B[:, 0:256], A.max), "N%d" % t, ["cw"], ["cm"])
+        vp(dv(256), lambda B: V.tensor_tensor(T.cn[:], T.cm[:], B[:, 256:512], A.min), "N%d" % t, ["cm"], ["cn"])
+        v(ds(256), lambda: V.tensor_copy(T.CAN[:].indirect(T[dwl][:]), T.cn[:]), ["cn", dwl], ["CAN", "CANd"])
+
+        def callsR(B):
+            r = [lambda: mm(B[:, 0:256], T.Ih[:], T.xw[:], True, False),
+                 lambda: mm(B[:, 0:256], T.Ih[:], T.Z[:, z0:z1], False, False),
+                 lambda: mm(B[:, 0:256], T.qtr[:], T.ones16[:], False, False)]
+            for h in range(2):
+                r.append(lambda h=h: mm(B[:, 128 * h:128 * h + 128], T.skrep[:, 128 * h:128 * h + 128], T.I5n[:], False, h == 1))
+            for h in range(2):
+                r.append(lambda h=h: mm(B[:, 256 + 128 * h:384 + 128 * h], T.skrep[:, 128 * h:128 * h + 128], T.Ib[:], True, True))
+            return r
+        op("t", pe(256, 256, 256, 128, 128, 128, 128), callsR, ["Ih", "xw", Z, "qtr", "ones16", "skrep", "I5n", "Ib"], [], tile="R%d" % t)
+        vp(dv(256), lambda B: V.tensor_tensor(T.r2m[:], T.r2[:], B[:, 256:512], A.mult), "R%d" % t, ["r2"], ["r2m"])
+        vp(dv(256), lambda B: V.tensor_tensor(T.rn[:], T.r2m[:], B[:, 0:256], A.max), "R%d" % t, ["r2m"], ["rn"])
+        v(ds(256), lambda: V.tensor_copy(T.X[:].indirect(T[dwu][:]), T.rn[:]), ["rn", dwu], XR)
+        v(ds(256), lambda: V.tensor_copy(T.X[:].indirect(T[dcu][:]), T[cutv][:]), [cutv, dcu], XR)
+
+    for t in range(NT):
+        step(t)
+
+    def store(name, out, src, R):
+        op("y", 0.1, [lambda: Y.dma_start(out, src)], R, ["y" + name], lat=3.0, sem="st_" + name, cnt=16)
+
+    s(sa(1024), lambda: S.activation(T.lo[:], T.CAN[:, 0:1024], AF.Identity, bias=2048.0, scale=-1.0), ["CAN"], ["lo"])
+    store("ol", T.yl[:], T.lo[:], ["lo"])
+    v(dv(256), lambda: ts(T.go[:], T["Gn%d" % (NT % 2)][:], -1.0, 2048.0, A.mult, A.add), ["Gn%d" % (NT % 2)], ["go"])
+    store("og", T.yg[:], T.go[:], ["go"])
+    for c in range(4):
+        a, b = 1024 * c, 1024 * c + 1024
+        if c < 3:
+            v(dh(1024), lambda a=a, b=b: ts(T.th[:, a:b], T.X[:, a:b], -BIAS, None, A.add), ["X%d" % c], ["th%d" % c])
+        else:
+            s(sa(1024), lambda a=a, b=b: S.activation(T.th[:, a:b], T.X[:, a:b], AF.Identity, bias=-BIAS), ["X%d" % c], ["th%d" % c])
+        store("o%d" % c, T.yx[:, a:b], T.th[:, a:b], ["th%d" % c])
+    emit(g, T, ops, schedule(ops))
+
+
+def depend(ops):
+    last, readers, tiles = {}, {}, {}
+    for o in ops:
+        d = set()
+        for r in o["R"]:
+            d.update(last.get(r, ()))
+        for w in o["W"]:
+            d.update(last.get(w, ()))
+            d.update(readers.get(w, ()))
+        for r in o["R"]:
+            readers.setdefault(r, []).append(o["i"])
+        for w in o["W"]:
+            last[w] = [o["i"]]
+            readers[w] = []
+        if o["tile"]:
+            tl = tiles.setdefault(o["tile"], [None, [], []])
+            if tl[0] != o["e"]:
+                tl[0], tl[1], tl[2] = o["e"], tl[2], []
+            d.update(tl[1])
+            tl[2].append(o["i"])
+        d.discard(o["i"])
+        o["d"] = d
+
+
+def schedule(ops):
+    depend(ops)
+    n = len(ops)
+    succ = [[] for _ in range(n)]
+    for o in ops:
+        for j in o["d"]:
+            succ[j].append(o["i"])
+    prio = [0.0] * n
+    for i in range(n - 1, -1, -1):
+        prio[i] = ops[i]["c"] + ops[i]["lat"] + SYNC + max([prio[j] for j in succ[i]] or [0.0])
+    users = {}
+    for o in ops:
+        if o["tile"]:
+            users.setdefault(o["tile"], []).append(o["i"])
+    left = {k: len(u) for k, u in users.items()}
+    bank = {}
+    free = {k: [] for k in range(8)}
+    need = [len(o["d"]) for o in ops]
+    rt, fin = [0.0] * n, [0.0] * n
+    ready = [i for i in range(n) if need[i] == 0]
+    et = {"v": 0.0, "s": 0.0, "t": 0.0, "g": 0.0, "y": 0.0, "x": 0.0}
+    order = []
+    while ready:
+        cand = []
+        for i in ready:
+            o = ops[i]
+            st = max(rt[i], et[o["e"]] if o["e"] != "x" else 0.0)
+            bk = None
+            if o["tile"] and o["tile"] not in bank:
+                if not free:
+                    continue
+                a, bk = min((max([fin[u] for u in us] or [0.0]), k) for k, us in free.items())
+                st = max(st, a + SYNC)
+            cand.append((st, -prio[i], i, bk))
+        if not cand:
+            raise ValueError("no bank for any ready op")
+        st, _, i, bk = min(cand, key=lambda c: c[:3])
+        ready.remove(i)
+        o = ops[i]
+        if bk is not None:
+            bank[o["tile"]] = bk
+            o["d"] = set(o["d"]) | set(free.pop(bk))
+        if o["tile"]:
+            o["b"] = bank[o["tile"]]
+            left[o["tile"]] -= 1
+            if left[o["tile"]] == 0:
+                free[o["b"]] = users[o["tile"]]
+        et[o["e"]] = st + o["c"]
+        fin[i] = st + o["c"] + o["lat"]
+        o["t0"] = st
+        order.append(i)
+        for j in succ[i]:
+            need[j] -= 1
+            rt[j] = max(rt[j], fin[i] + SYNC)
+            if need[j] == 0:
+                ready.append(j)
+    if len(order) != n:
+        raise ValueError("schedule stuck")
+    return order
+
+
+def emit(g, T, ops, order):
+    Q = {"v": g.vector, "s": g.scalar, "t": g.tensor, "g": g, "y": g.sync}
+    known = {e: {} for e in Q}
+    count, done = {}, {}
+    for i in order:
+        o = ops[i]
+        e = o["e"]
+        if e == "x":
+            done[i] = (o["sem"], o["cnt"], {})
+            continue
+        kn = known[e]
+        for _, j in sorted(((ops[j]["t0"], j) for j in o["d"]), reverse=True):
+            sm, c, snap = done[j]
+            if c > kn.get(sm, 0):
+                Q[e].wait_ge(T.sem[sm], c)
+                kn[sm] = c
+                for a, b in snap.items():
+                    if b > kn.get(a, 0):
+                        kn[a] = b
+        calls = o["f"](T["ps%d" % o["b"]]) if o["tile"] else o["f"]
+        for f in calls:
+            r = f()
+            if o["sem"] is None:
+                count["q" + e] = count.get("q" + e, 0) + 1
+                r.then_inc(T.sem["q" + e], 1)
+            elif not o["sem"].startswith("snt"):
+                r.then_inc(T.sem[o["sem"]], 16)
+        done[i] = (o["sem"] or "q" + e, o["cnt"] or count.get("q" + e, 0), dict(kn))
+    for sm in sorted(count):
+        g.wait_ge(T.sem[sm], count[sm])
+    for o in ops:
+        if o["sem"] is not None:
+            g.wait_ge(T.sem[o["sem"]], o["cnt"])

@@ -4,20 +4,20 @@ A = AluOpType
 AF = ActivationFunctionType
 NT = 8
 BIAS = 160.0
-XW = 5136
-CW = 1296
+XW = 6144
+CW = 1536
 
 F4, BF, HF, I4, U2 = "float32", "bfloat16", "float16", "int32", "uint16"
 SCRATCH = {}
 for _n, _s, _d in (
         ("X", XW, BF), ("CAN", CW, F4), ("cin", 1024, I4), ("tin", 256, I4), ("vin", 256, I4),
         ("xg0", 4096, BF), ("xg1", 4096, BF), ("ab", 4096, BF), ("th", 4096, BF), ("zrep", 4096, BF), ("sc", 4096, BF),
-        ("lo", 1024, F4), ("go", 256, F4), ("eqw", 3072, BF), ("eqc", 3072, BF), ("wrow", 2048, HF), ("wall", 2048, HF),
+        ("lo", 1024, F4), ("go", 256, F4), ("eqw", 3072, BF), ("eqc", 3072, BF), ("df", 3072, BF), ("wrow", 2048, HF), ("wall", 2048, HF),
         ("sco", 256, F4), ("q1", 16, I4), ("q2", 16, I4), ("UW", 256, HF), ("SPs", 256, HF), ("LwU", 32, F4),
         ("nw", 16, F4), ("n1w", 16, F4), ("nc", 16, F4), ("n1c", 16, F4), ("A1", 256, HF), ("A2c", 256, HF), ("A2w", 256, HF),
-        ("dwi", 16, I4), ("dws", 16, I4), ("uf", 16, HF), ("xs", 256, HF), ("xw", 256, BF), ("r2", 256, BF), ("r2m", 256, BF),
+        ("ufw", 16, HF), ("uf", 16, HF), ("xs", 256, HF), ("xw", 256, BF), ("r2", 256, BF), ("r2m", 256, BF),
         ("rn", 256, BF), ("cw", 256, F4), ("cm", 256, F4), ("cn", 256, F4), ("gm", 256, HF), ("sevL", 256, BF), ("sevT", 256, BF),
-        ("skrep", 256, BF), ("sf", 1, F4), ("si", 1, I4), ("s3", 1, I4), ("lim", 8, F4),
+        ("skrep", 256, BF), ("sf", 1, F4), ("si", 1, HF), ("sj", 16, F4), ("lim", 8, F4),
         ("Z", 256 * NT, BF), ("ZS", 256 * NT, BF),
         ("i128", 128, F4), ("pc", 1, F4), ("pci", 1, I4), ("pg", 1, F4), ("pk", 1, F4), ("p16", 1, F4),
         ("rc", 1, F4), ("k272", 272, F4), ("w144", 144, F4), ("v1", 256, F4), ("zli", 256, I4),
@@ -39,6 +39,14 @@ SEMAPHORES = (["qv", "qs", "qt", "qg"] + ["ld_" + n for n in ("cut", "z", "trail
               + ["arr%d" % k for k in range(1, NT)] + ["snt%d" % k for k in range(1, NT)])
 
 CY, GA, PEC, SYNC = 0.00083, 1.5, 0.0006, 0.1
+BONUS = {'cn_v': 1.5, 'dwu_v': 3, 'cnt_t': -1.5, 'zs_v': -1.5, 'nw_v': -0.7, 'SPs_v': 0.7, 'BCc_t': -6, 'sevL_v': 3, 'Aw_v': -1.5,
+         'd_t': -3, 'X_v': -6, 'gm_v': -3, 'eqc_v': -3, 'N_t': -6, 'vl_v': -1.5, 'UW_v': -1.5, 'wrow_y': 1.5, 'th_v': -0.7, 'lim_v': 6,
+         'A_v': 6, 'Gu_v': -3, 'sc_v': 3, 'sco_v': 3, 'ab_s': 3, 'eqw_v': 3, 'xw_s': -0.7, 'Ku_v': 3, 'cw_v': 3, 'r_v': -3,
+         'zrep_s': -1.5, 'si_v': -6, 'uf_v': -0.7, 'Ibn_v': 6, 'SP_t': 3, 'cm_v': 1.5, 'cw_s': 0.7, 'rn_v': 6, 'lo_v': 3, 'CAN_v': -3,
+         'R_t': -3, 'xg_s': -3, 'Ww_t': 3, 'Ac_v': -3, 'Lc_v': 0.7, 'nc_v': 6, 'Z_x': -0.7, 'S_t': -3, 'sf_s': -1.5, 'cu_v': -0.7,
+         'wall_g': -3, 'Gn_v': -3, 'key_t': 0.7, 'dwl_v': 1.5, 'Wc_t': 0.7, 'cutv_s': -3, 'Z_v': -3, 'q_v': -1.5, 'EQw_t': 3,
+         'EQc_t': -1.5, 'cW_t': 6, 'rm_v': 1.5, 'df_s': 0.7, 'sevT_v': 3, 'way_g': -3, 'xs_v': 0.7, 'G_t': -3}
+EA = (0, 1, 2)
 
 
 def dv(n): return 0.06 + n * CY
@@ -75,8 +83,8 @@ def rank_program(g, core, T, topo):
         op("y", 0.1, [lambda: Y.dma_start(out, src)], R, W, lat=lat, sem="ld_" + name, cnt=16)
 
     v(dv(256), lambda: V.memset(T.vin[:], 0), [], ["vin"])
-    v(dv(512), lambda: V.memset(T.X[:, 4096:XW], BIAS), [], ["Xd"])
-    v(dv(272), lambda: V.memset(T.CAN[:, 1024:CW], 0.0), [], ["CANd"])
+    v(dh(2048), lambda: V.memset(T.X[:, 4096:XW], BIAS), [], ["Xd"])
+    v(dv(512), lambda: V.memset(T.CAN[:, 1024:CW], 0.0), [], ["CANd"])
     load("z", T.xw[:], T.z[:], ["xw"], 2.0)
     load("trail", T.tin[:], T.trail[:], ["tin"], 2.2)
     load("canal", T.cin[:], T.canal[:], ["cin"], 4.0)
@@ -98,7 +106,7 @@ def rank_program(g, core, T, topo):
     iota("i128", T.i128[:], [[1, 128]], 0, 0)
     iota("k272", T.k272[:], [[0, 17], [1, 16]], 0, 0)
     iota("zli", T.zli[:], [[1, 256]], 0, 0, False)
-    iota("v1", T.v1[:], [[-512, 2], [0, 128]], -2052, -4)
+    iota("v1", T.v1[:], [[-1024, 2], [0, 128]], -2052, -8)
     iota("w144", T.w144[:], [[1, 144]], -15, 0)
     iota("sklia", T.skli[:, 0:64], [[1, 4], [16, 16]], 12, 0, False)
     iota("sklib", T.skli[:, 64:128], [[1, 4], [16, 16]], 0, 0, False)
@@ -117,7 +125,7 @@ def rank_program(g, core, T, topo):
         v(dv(128), lambda name=name, val=val: ts(T[name][:], T.i128[:], T.pc[:], val, A.is_equal, A.mult), ["i128", "pc"], [name])
     for name, val in (("blkf", 1.0), ("blk1", 1.0), ("blkb", 1.0), ("blkS", 4096.0)):
         v(one, lambda name=name, val=val: ts(T[name][:], T.i128[:, 0:8], T.pg[:], val, A.is_equal, A.mult), ["i128", "pg"], [name])
-    v(dh(256), lambda: V.tensor_scalar(T.ones16[:], T.k272[:, 0:256], 0.0, 1.0, A.mult, A.add), ["k272"], ["ones16"])
+    v(dv(256), lambda: ts(T.ones16[:], T.k272[:, 0:256], 0.0, 1.0, A.mult, A.add), ["k272"], ["ones16"])
     v(dh(128), lambda: V.memset(T.onesb[:], 1.0), [], ["onesb"])
     v(dh(128), lambda: ts(T.qtr[:], T.ones16[:, 0:128], -0.25 / 128, None, A.mult), ["ones16"], ["qtr"])
     v(one, lambda: V.memset(T.wbig[:], float(2.0 ** 90)), [], ["wbig"])
@@ -172,12 +180,22 @@ def rank_program(g, core, T, topo):
             def cmp(W, off, k, h):
                 return lambda: ts(T[eq][:, 384 * k + 256 * h:384 * k + 256 + 128 * h], W[:, off + 128 * h:off + 256],
                                   T[Lname][:, col0 + 8 * h + k:col0 + 8 * h + k + 1], None, A.is_equal)
+
+            def dist(B, k, h):
+                return lambda: S.activation(T.df[:, 384 * k + 256 * h:384 * k + 256 + 128 * h], B[:, 256 * (k % 2) + 128 * h:256 * (k % 2) + 256],
+                                            AF.Abs, bias=T[Lname][:, col0 + 8 * h + k:col0 + 8 * h + k + 1], scale=-1.0)
             if pb:
                 op("v", 2 * dh(256) + 2 * dh(128), [cmp(T.wall, 256 * k, k, h) for k in ks for h in range(2)], [Lname, "wall"], ["%s_%d" % (eq, b)])
+                continue
+            tn = "BC%s%d_%d" % (tag, t, b)
+            op("t", pe(256, 256), lambda B, ks=ks: [lambda k=k: mm(B[:, 256 * (k % 2):256 * (k % 2) + 256], T.onesg[:, 128 * k:128 * k + 128],
+               T[src][:], True, True) for k in ks], [src, "onesg"], [], tile=tn)
+            if b in EA:
+                op("s", 2 * sa(256) + 2 * sa(128), lambda B, ks=ks, dist=dist: [dist(B, k, h) for k in ks for h in range(2)],
+                   [Lname], ["df_%d" % b], tile=tn)
+                v(dh(768), lambda b=b: ts(T[eq][:, 768 * b:768 * b + 768], T.df[:, 768 * b:768 * b + 768], 0.0, None, A.is_equal),
+                  ["df_%d" % b], ["%s_%d" % (eq, b)])
             else:
-                tn = "BC%s%d_%d" % (tag, t, b)
-                op("t", pe(256, 256), lambda B, ks=ks: [lambda k=k: mm(B[:, 256 * (k % 2):256 * (k % 2) + 256], T.onesg[:, 128 * k:128 * k + 128],
-                   T[src][:], True, True) for k in ks], [src, "onesg"], [], tile=tn)
                 op("v", 2 * dv(256) + 2 * dv(128), lambda B, ks=ks, cmp=cmp: [cmp(B, 256 * (k % 2), k, h) for k in ks for h in range(2)],
                    [Lname], ["%s_%d" % (eq, b)], tile=tn)
         tn = "EQ%s%d" % (tag, t)
@@ -236,10 +254,9 @@ def rank_program(g, core, T, topo):
         v(one, lambda: V.tensor_tensor(T.n1w[:], T.nw[:], T.LwU[:, 0:16], A.add), ["nw", "LwU"], ["n1w"])
         v(dg(256), lambda: V.tensor_tensor(T.A2w[:], T.n1w[:, 0:16].indirect(T.zl[:, 0:16]), T.in1c[:], A.max), ["n1w", "zl", "in1c"], ["A2w"])
         spread_lists("A2w", "W2w%d" % t)
-        vp(one, lambda B: ts(T.dwi[:], B[:, 0:16], -1.0, 63488.0, A.mult, A.add), "W2w%d" % t, [], ["dwi"])
-        v(one, lambda: V.tensor_copy(T[dwu][:], T.dwi[:]), ["dwi"], [dwu])
-        v(one, lambda: ts(T.dws[:], T.dwi[:], 2, None, A.arith_shift_right), ["dwi"], ["dws"])
-        v(one, lambda: V.tensor_copy(T[dwl][:], T.dws[:]), ["dws"], [dwl])
+        vp(one, lambda B: ts(T[dwu][:], B[:, 0:16], -1.0, 63488.0, A.mult, A.add), "W2w%d" % t, [], [dwu])
+        vp(one, lambda B: ts(T.ufw[:], B[:, 0:16], -0.25, 16896.625, A.mult, A.add), "W2w%d" % t, [], ["ufw"])
+        v(one, lambda: ts(T[dwl][:], T.ufw[:], -1025.0, None, A.add), ["ufw"], [dwl])
         s(sg(256), lambda: S.activation(T.xw[:], T.X[:].indirect(T[dwu][:]), AF.Copy), XR + [dwu], ["xw"])
         s(sg(256), lambda: S.activation(T.cw[:], T.CAN[:].indirect(T[dwl][:]), AF.Copy), ["CAN", "CANd", dwl], ["cw"])
         v(dh(256), lambda: ts(T.r2[:], T.xw[:], 4.0, BIAS + 63.0, A.add, A.min), ["xw"], ["r2"])
@@ -283,32 +300,34 @@ def rank_program(g, core, T, topo):
         vp(one, lambda B: ts(T[dcu][:], B[:, 0:16], -1.0, 63488.0, A.mult, A.add), "W2c%d" % t, [], [dcu])
         for b in range(8):
             tn = "d%d_%d" % (t, b)
+            h, kb = b // 4, 4 * (b % 4)
 
-            def callsD(B, b=b):
+            def callsD(B, h=h, kb=kb):
                 r = []
-                for j in range(2):
-                    r.append(lambda j=j: mm(B[:, 256 * j:256 * j + 256], T.Ib[:], T[xg][:, 2 * b + j:4096:16], True, False))
-                    r.append(lambda j=j: mm(B[:, 256 * j:256 * j + 256], T.Ibn[:], T.Z[:, z0:z1], False, True))
+                for j in range(4):
+                    r.append(lambda j=j: mm(B[:, 128 * j:128 * j + 128], T.Ib[:], T[xg][:, 2048 * h + kb + j:2048 * h + 2048:16], True, False))
+                    r.append(lambda j=j: mm(B[:, 128 * j:128 * j + 128], T.Ibn[:], T.Z[:, z0 + 128 * h:z0 + 128 * h + 128], False, True))
                 return r
-            op("t", pe(256, 256, 256, 256), callsD, ["Ib", "Ibn", Z] + ["%s_%d" % (xg, c) for c in range(4)], [], tile=tn)
+            op("t", pe(*([128] * 8)), callsD, ["Ib", "Ibn", Z] + ["%s_%d" % (xg, c) for c in (2 * h, 2 * h + 1)], [], tile=tn)
             op("s", sa(512), lambda B, b=b: [lambda: S.activation(T.ab[:, 512 * b:512 * b + 512], B[:], AF.Abs)], [], ["ab%d" % b], tile=tn)
             if b % 2 == 1:
                 c = b // 2
                 v(dh(1024), lambda c=c: ts(T.th[:, 1024 * c:1024 * c + 1024], T.ab[:, 1024 * c:1024 * c + 1024], T.lim[:, t:t + 1], None, A.is_gt),
                   ["ab%d" % (b - 1), "ab%d" % b, "lim%d" % t], ["th%d" % c])
         for c in range(4):
-            op("t", pe(*([64] * 8)), lambda B, c=c: [
-                lambda k=k, h=h: mm(B[:, 128 * h + k:128 * h + 128:16], T.th[:, 256 * k + 128 * h:256 * k + 128 * h + 128], T.blkb[:], True, True)
-                for k in range(4 * c, 4 * c + 4) for h in range(2)], ["th%d" % c, "blkb"], [], tile="cnt%d" % t)
+            h = c // 2
+            op("t", pe(*([64] * 8)), lambda B, c=c, h=h: [
+                lambda k=k: mm(B[:, 128 * h + k:128 * h + 128:16], T.th[:, 2048 * h + 128 * k:2048 * h + 128 * k + 128], T.blkb[:], True, True)
+                for k in range(8 * (c % 2), 8 * (c % 2) + 8)], ["th%d" % c, "blkb"], [], tile="cnt%d" % t)
         vp(dv(256), lambda B: ts(T.sevL[:], B[:, 0:256], 8.5, None, A.is_gt), "cnt%d" % t, [], ["sevL"])
         vp(dv(256), lambda B: V.tensor_tensor(T.sevT[:], B[:, 0:256], T.thrk[:, 15 - t:271 - t], A.is_gt), "cnt%d" % t, ["thrk"], ["sevT"])
         s(sg(256), lambda: S.activation(T.skrep[:], T.sevL[:].indirect(T.skl[:, 16 * t:16 * t + 16]), AF.Copy), ["sevL", "skl"], ["skrep"])
         if not last:
             op("t", pe(64), lambda B: [lambda: mm(B[:, 0:16], T.onesb[:], T.sevL[:, k0:256:16], True, True)], ["onesb", "sevL"], [], tile="S%d" % t)
-            vp(one, lambda B: V.tensor_reduce(T.sf[:], B[:, 0:16], AxisListType.X, A.add), "S%d" % t, [], ["sf"])
-            v(one, lambda: V.tensor_copy(T.si[:], T.sf[:]), ["sf"], ["si"])
-            v(one, lambda: ts(T.s3[:], T.si[:], 3, None, A.bitwise_and), ["si"], ["s3"])
-            v(one, lambda: ts(T.lim[:, t + 1:t + 2], T.s3[:], 16.0, None, A.add), ["s3"], ["lim%d" % (t + 1)])
+            op("s", sa(16) + 0.14, lambda B: [lambda: S.activation(T.sj[:], B[:, 0:16], AF.Identity, bias=385.0, accum_out=T.sf[:])],
+               [], ["sf"], tile="S%d" % t)
+            v(one, lambda: ts(T.si[:], T.sf[:], 0.25, -4.375, A.mult, A.add), ["sf"], ["si"])
+            v(one, lambda: ts(T.lim[:, t + 1:t + 2], T.si[:], -4.0, T.sf[:], A.mult, A.add), ["si", "sf"], ["lim%d" % (t + 1)])
 
         def blend(ident, extra, sevs):
             def calls(B):
@@ -403,6 +422,8 @@ def schedule(ops):
     prio = [0.0] * n
     for i in range(n - 1, -1, -1):
         prio[i] = ops[i]["c"] + ops[i]["lat"] + SYNC + max([prio[j] for j in succ[i]] or [0.0])
+    for o in ops:
+        prio[o["i"]] += BONUS.get("".join(c for c in (o["W"] or [o["tile"]])[0] if c.isalpha()) + "_" + o["e"], 0.0)
     users = {}
     for o in ops:
         if o["tile"]:

from concourse.mybir import AluOpType, AxisListType, ActivationFunctionType

A = AluOpType
AF = ActivationFunctionType
NT = 8
BIAS = 160.0
XW = 6144
CW = 1536

F4, BF, HF, I4, U2 = "float32", "bfloat16", "float16", "int32", "uint16"
SCRATCH = {}
for _n, _s, _d in (
        ("X", XW, BF), ("CAN", CW, F4), ("cin", 1024, I4), ("tin", 256, I4), ("vin", 256, I4),
        ("xg0", 4096, BF), ("xg1", 4096, BF), ("ab", 4096, BF), ("th", 4096, BF), ("zrep", 4096, BF), ("sc", 4096, BF),
        ("lo", 1024, F4), ("go", 256, F4), ("eqw", 3072, BF), ("eqc", 3072, BF), ("df", 3072, BF), ("wrow", 2048, HF), ("wall", 2048, HF),
        ("sco", 256, F4), ("q1", 16, I4), ("q2", 16, I4), ("UW", 256, HF), ("SPs", 256, HF), ("LwU", 32, F4),
        ("nw", 16, F4), ("n1w", 16, F4), ("nc", 16, F4), ("n1c", 16, F4), ("A1", 256, HF), ("A2c", 256, HF), ("A2w", 256, HF),
        ("ufw", 16, HF), ("uf", 16, HF), ("xs", 256, HF), ("xw", 256, BF), ("r2", 256, BF), ("r2m", 256, BF),
        ("rn", 256, BF), ("cw", 256, F4), ("cm", 256, F4), ("cn", 256, F4), ("gm", 256, HF), ("sevL", 256, BF), ("sevT", 256, BF),
        ("skrep", 256, BF), ("sf", 1, F4), ("si", 1, HF), ("sj", 16, F4), ("lim", 8, F4),
        ("Z", 256 * NT, BF), ("ZS", 256 * NT, BF),
        ("i128", 128, F4), ("pc", 1, F4), ("pci", 1, I4), ("pg", 1, F4), ("pk", 1, F4), ("p16", 1, F4),
        ("rc", 1, F4), ("k272", 272, F4), ("w144", 144, F4), ("v1", 256, F4), ("zli", 256, I4),
        ("skli", 128, I4), ("zl", 256, U2), ("skl", 128, U2), ("RM", 16, F4), ("RM1", 16, F4), ("RM2", 16, F4), ("RMn", 16, F4),
        ("I16", 128, HF), ("I8n", 128, BF), ("I8p", 128, BF), ("Ib", 128, BF), ("Ibn", 128, BF), ("Ih", 128, BF), ("I5n", 128, BF),
        ("It", 1024, HF), ("blkf", 8, F4), ("blk1", 8, HF), ("blkb", 8, BF), ("blkS", 8, BF), ("onesg", 1024, HF), ("ones16", 256, HF),
        ("onesb", 128, BF), ("qtr", 128, HF), ("dmask", 256, HF), ("in1c", 256, HF), ("selk", 64, HF), ("wide", 144, HF),
        ("thrk", 272, F4), ("resetv", 256, F4), ("wtf", 1, F4), ("wt", 1, BF), ("wbig", 1, BF), ("thr", 1, F4)):
    SCRATCH[_n] = ("sbuf", [128, _s], _d)
for _k in range(2):
    for _n, _s, _d in (("Kn", 256, HF), ("Ku", 256, U2), ("Gn", 256, HF), ("Gu", 256, U2), ("cutv", 256, BF), ("Lc", 16, F4),
                       ("cu", 16, U2), ("vl", 16, U2), ("dwu", 16, U2), ("dwl", 16, U2), ("dcu", 16, U2)):
        SCRATCH["%s%d" % (_n, _k)] = ("sbuf", [128, _s], _d)
for _k in range(8):
    SCRATCH["ps%d" % _k] = ("psum", [128, 512], F4)

SEMAPHORES = (["qv", "qs", "qt", "qg"] + ["ld_" + n for n in ("cut", "z", "trail", "canal", "x0", "x1", "x2", "x3")]
              + ["st_" + n for n in ("o0", "o1", "o2", "o3", "ol", "og")] + ["row%d" % k for k in range(NT)]
              + ["arr%d" % k for k in range(1, NT)] + ["snt%d" % k for k in range(1, NT)])

CY, GA, PEC, SYNC = 0.00083, 1.5, 0.0006, 0.1
BONUS = {'cn_v': 1.5, 'dwu_v': 3, 'cnt_t': -1.5, 'zs_v': -1.5, 'nw_v': -0.7, 'SPs_v': 0.7, 'BCc_t': -6, 'sevL_v': 3, 'Aw_v': -1.5,
         'd_t': -3, 'X_v': -6, 'gm_v': -3, 'eqc_v': -3, 'N_t': -6, 'vl_v': -1.5, 'UW_v': -1.5, 'wrow_y': 1.5, 'th_v': -0.7, 'lim_v': 6,
         'A_v': 6, 'Gu_v': -3, 'sc_v': 3, 'sco_v': 3, 'ab_s': 3, 'eqw_v': 3, 'xw_s': -0.7, 'Ku_v': 3, 'cw_v': 3, 'r_v': -3,
         'zrep_s': -1.5, 'si_v': -6, 'uf_v': -0.7, 'Ibn_v': 6, 'SP_t': 3, 'cm_v': 1.5, 'cw_s': 0.7, 'rn_v': 6, 'lo_v': 3, 'CAN_v': -3,
         'R_t': -3, 'xg_s': -3, 'Ww_t': 3, 'Ac_v': -3, 'Lc_v': 0.7, 'nc_v': 6, 'Z_x': -0.7, 'S_t': -3, 'sf_s': -1.5, 'cu_v': -0.7,
         'wall_g': -3, 'Gn_v': -3, 'key_t': 0.7, 'dwl_v': 1.5, 'Wc_t': 0.7, 'cutv_s': -3, 'Z_v': -3, 'q_v': -1.5, 'EQw_t': 3,
         'EQc_t': -1.5, 'cW_t': 6, 'rm_v': 1.5, 'df_s': 0.7, 'sevT_v': 3, 'way_g': -3, 'xs_v': 0.7, 'G_t': -3}
EA = (0, 1, 2)


def dv(n): return 0.06 + n * CY
def dh(n): return 0.06 + max(n * 0.5, 64) * CY
def dg(n): return 0.05 + n * GA * CY
def ds(n): return 0.05 + n * 3.5 * CY
def sg(n): return 0.065 + n * GA * CY
def sa(n): return 0.065 + n * CY
def pe(*ns): return sum(max(64, n) for n in ns) * PEC + 0.02


def rank_program(g, core, T, topo):
    rank = T.rank_of(core)
    if rank is None:
        return
    V, S, PE, Y = g.vector, g.scalar, g.tensor, g.sync
    ops = []

    def op(eng, cost, calls, R=(), W=(), tile=None, lat=0.0, sem=None, cnt=0):
        ops.append({"e": eng, "c": cost, "f": calls, "R": list(R), "W": list(W), "tile": tile, "lat": lat,
                    "sem": sem, "cnt": cnt, "i": len(ops)})

    def v(cost, f, R, W): op("v", cost, [f], R, W)
    def s(cost, f, R, W): op("s", cost, [f], R, W)
    def vp(cost, f, tile, R, W): op("v", cost, lambda B: [lambda: f(B)], R, W, tile=tile)
    mm = PE.matmul

    def ts(out, i0, s1, s2, o0, o1=None):
        if o1 is None:
            return V.tensor_scalar(out, i0, s1, None, o0)
        return V.tensor_scalar(out, i0, s1, s2, o0, o1)

    def load(name, out, src, W, lat, R=()):
        op("y", 0.1, [lambda: Y.dma_start(out, src)], R, W, lat=lat, sem="ld_" + name, cnt=16)

    v(dv(256), lambda: V.memset(T.vin[:], 0), [], ["vin"])
    v(dh(2048), lambda: V.memset(T.X[:, 4096:XW], BIAS), [], ["Xd"])
    v(dv(512), lambda: V.memset(T.CAN[:, 1024:CW], 0.0), [], ["CANd"])
    load("z", T.xw[:], T.z[:], ["xw"], 2.0)
    load("trail", T.tin[:], T.trail[:], ["tin"], 2.2)
    load("canal", T.cin[:], T.canal[:], ["cin"], 4.0)
    for q in range(4):
        load("x%d" % q, T.X[:, 1024 * q:1024 * q + 1024], T.x[:, 1024 * q:1024 * q + 1024], ["X%d" % q], 4.0 + q)
    load("cut", T.vin[0:128:16, :], T.cut[:], ["vin2"], 2.0, ["vin"])
    XC = ["X0", "X1", "X2", "X3"]
    XR = XC + ["Xd"]

    def iota(name, out, pat, base, cm, f=True):
        n = 1
        for a, b in pat:
            n *= b
        kw = {"allow_small_or_imprecise_dtypes": True} if f else {}
        op("g", 0.13 + 2 * n * CY, [lambda: g.iota(out, pat, base, cm, **kw)], [], [name])

    iota("pci", T.pci[:], [[0, 1]], 0, 1, False)
    iota("pc", T.pc[:], [[0, 1]], 0, 1)
    iota("i128", T.i128[:], [[1, 128]], 0, 0)
    iota("k272", T.k272[:], [[0, 17], [1, 16]], 0, 0)
    iota("zli", T.zli[:], [[1, 256]], 0, 0, False)
    iota("v1", T.v1[:], [[-1024, 2], [0, 128]], -2052, -8)
    iota("w144", T.w144[:], [[1, 144]], -15, 0)
    iota("sklia", T.skli[:, 0:64], [[1, 4], [16, 16]], 12, 0, False)
    iota("sklib", T.skli[:, 64:128], [[1, 4], [16, 16]], 0, 0, False)
    one = dv(64)
    v(one, lambda: ts(T.q1[:, 0:1], T.pci[:], 4, None, A.arith_shift_right), ["pci"], ["q1"])
    v(one, lambda: ts(T.q2[:, 0:1], T.pci[:], 15, None, A.bitwise_and), ["pci"], ["q2"])
    v(one, lambda: V.tensor_copy(T.pg[:], T.q1[:, 0:1]), ["q1"], ["pg"])
    v(one, lambda: V.tensor_copy(T.pk[:], T.q2[:, 0:1]), ["q2"], ["pk"])
    v(one, lambda: ts(T.p16[:], T.pg[:], 16.0, None, A.mult), ["pg"], ["p16"])
    v(one, lambda: ts(T.rc[:], T.pk[:], 0.0, 2048.0, A.is_equal, A.mult), ["pk"], ["rc"])
    v(one, lambda: ts(T.RM[:], T.i128[:, 0:16], T.pk[:], None, A.is_equal), ["i128", "pk"], ["RM"])
    v(one, lambda: ts(T.RM1[:], T.RM[:], 0.25, None, A.mult), ["RM"], ["RM1"])
    v(one, lambda: ts(T.RM2[:], T.RM[:], 1536.375, None, A.mult), ["RM"], ["RM2"])
    v(one, lambda: ts(T.RMn[:], T.RM[:], -1.0, 1.0, A.mult, A.add), ["RM"], ["RMn"])
    for name, val in (("I16", 1.0), ("Ib", 1.0), ("Ibn", -1.0), ("I8n", -8192.0), ("I8p", 8192.0), ("Ih", 0.5), ("I5n", -512.0)):
        v(dv(128), lambda name=name, val=val: ts(T[name][:], T.i128[:], T.pc[:], val, A.is_equal, A.mult), ["i128", "pc"], [name])
    for name, val in (("blkf", 1.0), ("blk1", 1.0), ("blkb", 1.0), ("blkS", 4096.0)):
        v(one, lambda name=name, val=val: ts(T[name][:], T.i128[:, 0:8], T.pg[:], val, A.is_equal, A.mult), ["i128", "pg"], [name])
    v(dv(256), lambda: ts(T.ones16[:], T.k272[:, 0:256], 0.0, 1.0, A.mult, A.add), ["k272"], ["ones16"])
    v(dh(128), lambda: V.memset(T.onesb[:], 1.0), [], ["onesb"])
    v(dh(128), lambda: ts(T.qtr[:], T.ones16[:, 0:128], -0.25 / 128, None, A.mult), ["ones16"], ["qtr"])
    v(one, lambda: V.memset(T.wbig[:], float(2.0 ** 90)), [], ["wbig"])
    v(one, lambda: V.memset(T.lim[:, 0:1], 16.0), [], ["lim0"])
    op("v", 8 * dh(128), [lambda k=k: ts(T.onesg[:, 128 * k:128 * k + 128], T.ones16[:, 0:128], T.blkf[:, k:k + 1], None, A.mult)
                          for k in range(8)], ["ones16", "blkf"], ["onesg"])
    v(dv(256), lambda: ts(T.dmask[:], T.k272[:, 0:256], T.pk[:], None, A.is_equal), ["k272", "pk"], ["dmask"])
    v(dv(256), lambda: ts(T.resetv[:], T.k272[:, 0:256], 0.0, -2.0e7, A.is_equal, A.mult), ["k272"], ["resetv"])
    v(dv(272), lambda: ts(T.sco[:], T.v1[:], -4096.0, None, A.add), ["v1"], ["sco"])
    v(dv(512), lambda: V.tensor_tensor(T.go[:], T.sco[:], T.dmask[:], A.mult), ["sco", "dmask"], ["go"])
    v(dv(256), lambda: ts(T.in1c[:], T.go[:], 4096.0, None, A.add), ["go"], ["in1c"])
    v(dv(272), lambda: ts(T.thrk[:], T.k272[:], 15.0, 100.0, A.is_equal, A.mult), ["k272"], ["thrk0"])
    v(dv(272), lambda: ts(T.thrk[:], T.thrk[:], 8.5, None, A.add), ["thrk0"], ["thrk"])
    v(dv(144), lambda: ts(T.wide[:], T.w144[:], T.p16[:], None, A.is_equal), ["w144", "p16"], ["wide"])
    v(dv(256), lambda: V.tensor_copy(T.zl[:], T.zli[:]), ["zli"], ["zl"])
    v(dv(128), lambda: V.tensor_copy(T.skl[:], T.skli[:]), ["sklia", "sklib"], ["skl"])
    op("v", 8 * one, [lambda t=t: ts(T.selk[:, 8 * t:8 * t + 8], T.blkf[:], T.RM[:, (t + 12) % 16:(t + 12) % 16 + 1], None, A.mult)
                      for t in range(NT)], ["blkf", "RM"], ["selk"])
    op("v", 8 * dh(128), [lambda t=t: ts(T.It[:, 128 * t:128 * t + 128], T.I16[:], T.RMn[:, t:t + 1], None, A.mult)
                          for t in range(NT)], ["I16", "RMn"], ["It"])
    v(dv(128), lambda: V.memset(T.cm[:, 0:128], 0.5), [], ["cm"])
    v(dv(128), lambda: V.memset(T.cn[:, 0:128], 0.0), [], ["cn"])
    v(dv(128), lambda: V.tensor_tensor_scan(T.cw[:, 0:128], T.cm[:, 0:128], T.cn[:, 0:128], float(2.0 ** 64), A.mult, A.add), ["cm", "cn"], ["cw"])
    v(dv(256), lambda: V.tensor_tensor(T.lo[:, 0:128], T.cw[:, 0:128], T.I16[:], A.mult), ["cw", "I16"], ["lo"])
    v(dv(128), lambda: V.tensor_reduce(T.wtf[:], T.lo[:, 0:128], AxisListType.X, A.add), ["lo"], ["wtf"])
    v(one, lambda: V.tensor_copy(T.wt[:], T.wtf[:]), ["wtf"], ["wt"])
    v(one, lambda: ts(T.thr[:], T.wtf[:], 2.5, None, A.mult), ["wtf"], ["thr"])

    v(dv(256), lambda: ts(T.UW[:], T.vin[:], -1.0, T.rc[:], A.mult, A.add), ["vin", "vin2", "rc"], ["UW"])
    v(dv(256), lambda: ts(T.Gn0[:], T.tin[:], -1.0, 2048.0, A.mult, A.add), ["tin"], ["Gn0"])
    v(dv(256), lambda: V.tensor_copy(T.Gu0[:], T.tin[:]), ["tin"], ["Gu0"])
    v(dh(256), lambda: ts(T.Z[:, 0:256], T.xw[:], BIAS, None, A.add), ["xw"], ["Z0"])
    v(dv(1024), lambda: ts(T.CAN[:, 0:1024], T.cin[:], -1.0, 2048.0, A.mult, A.add), ["cin"], ["CAN"])
    for q in range(4):
        v(dh(1024), lambda q=q: ts(T.X[:, 1024 * q:1024 * q + 1024], T.X[:, 1024 * q:1024 * q + 1024], BIAS, None, A.add),
          ["X%d" % q], ["X%d" % q])

    def halves(src, rhs):
        return lambda B: [lambda h=h: mm(B[:, 8 * h:8 * h + 8], T[src][:, 128 * h:128 * h + 128], rhs, True, True) for h in range(2)]

    def spread_lists(key, tname):
        op("t", pe(64, 64), halves(key, T.blk1[:]), [key, "blk1"], [], tile=tname)

    def same(t, tag, src, col0, Lname, eq, pb):
        k0 = (t + 12) % 16
        if pb:
            op("y", 0.1, [lambda: Y.dma_start(T.wrow[0:1, :], T[src][k0:128:16, :])], [src], ["wrow"], lat=2.0, sem="row%d" % t, cnt=16)
            op("g", 0.14 + 4 * 2048 * CY, [lambda: g.partition_broadcast(T.wall[:], T.wrow[0:1, :], 128)], ["wrow"], ["wall"])
        for b in range(4):
            ks = (2 * b, 2 * b + 1)

            def cmp(W, off, k, h):
                return lambda: ts(T[eq][:, 384 * k + 256 * h:384 * k + 256 + 128 * h], W[:, off + 128 * h:off + 256],
                                  T[Lname][:, col0 + 8 * h + k:col0 + 8 * h + k + 1], None, A.is_equal)

            def dist(B, k, h):
                return lambda: S.activation(T.df[:, 384 * k + 256 * h:384 * k + 256 + 128 * h], B[:, 256 * (k % 2) + 128 * h:256 * (k % 2) + 256],
                                            AF.Abs, bias=T[Lname][:, col0 + 8 * h + k:col0 + 8 * h + k + 1], scale=-1.0)
            if pb:
                op("v", 2 * dh(256) + 2 * dh(128), [cmp(T.wall, 256 * k, k, h) for k in ks for h in range(2)], [Lname, "wall"], ["%s_%d" % (eq, b)])
                continue
            tn = "BC%s%d_%d" % (tag, t, b)
            op("t", pe(256, 256), lambda B, ks=ks: [lambda k=k: mm(B[:, 256 * (k % 2):256 * (k % 2) + 256], T.onesg[:, 128 * k:128 * k + 128],
               T[src][:], True, True) for k in ks], [src, "onesg"], [], tile=tn)
            if b in EA:
                op("s", 2 * sa(256) + 2 * sa(128), lambda B, ks=ks, dist=dist: [dist(B, k, h) for k in ks for h in range(2)],
                   [Lname], ["df_%d" % b], tile=tn)
                v(dh(768), lambda b=b: ts(T[eq][:, 768 * b:768 * b + 768], T.df[:, 768 * b:768 * b + 768], 0.0, None, A.is_equal),
                  ["df_%d" % b], ["%s_%d" % (eq, b)])
            else:
                op("v", 2 * dv(256) + 2 * dv(128), lambda B, ks=ks, cmp=cmp: [cmp(B, 256 * (k % 2), k, h) for k in ks for h in range(2)],
                   [Lname], ["%s_%d" % (eq, b)], tile=tn)
        tn = "EQ%s%d" % (tag, t)
        for b in range(4):
            def sums(B, b=b):
                r = []
                for k in (2 * b, 2 * b + 1):
                    o = 384 * k
                    r.append(lambda k=k, o=o: mm(B[:, k:k + 1], T[eq][:, o:o + 128], T.wt[:], True, True))
                    r.append(lambda k=k, o=o: mm(B[:, 8 + k:9 + k], T[eq][:, o + 128:o + 256], T.wbig[:], True, False))
                    r.append(lambda k=k, o=o: mm(B[:, 8 + k:9 + k], T[eq][:, o + 256:o + 384], T.wt[:], False, True))
                return r
            op("t", pe(64, 64, 64, 64, 64, 64), sums, ["%s_%d" % (eq, b), "wt", "wbig"], [], tile=tn)
        return tn

    def place(t, par, first):
        v(dg(256), lambda: V.tensor_tensor(T.A1[:], T["Lc%d" % par][:, 0:16].indirect(T.zl[:, 0:16]), T.dmask[:], A.mult),
          ["Lc%d" % par, "zl", "dmask"], ["A1"])
        tn = "cW%d" % t
        spread_lists("A1", tn)
        if not first:
            vp(one, lambda B: ts(T["cu%d" % par][:], B[:, 0:16], -1.0, 2048.0, A.mult, A.add), tn, [], ["cu%d" % par])
        if t < NT - 1:
            vp(one, lambda B: ts(T.uf[:], B[:, 0:16], 0.25, 1536.375, A.mult, A.add), tn, [], ["uf"])
            v(one, lambda: ts(T["vl%d" % par][:], T.uf[:], -1.0, 2048.0, A.mult, A.add), ["uf"], ["vl%d" % par])

    op("t", pe(64, 64), halves("UW", T.blk1[:]), ["UW", "blk1"], [], tile="cut0")
    vp(one, lambda B: V.tensor_copy(T.Lc1[:], B[:, 0:16]), "cut0", [], ["Lc1"])
    place(-1, 1, True)

    def step(t):
        p, q = t % 2, 1 - t % 2
        last = t == NT - 1
        k0 = (t + 12) % 16
        Z, Kn, Ku, Gn, Gu, xg = "Z%d" % t, "Kn%d" % p, "Ku%d" % p, "Gn%d" % p, "Gu%d" % p, "xg%d" % p
        Lc, cu, dcu, dwu, dwl, cutv = "Lc%d" % p, "cu%d" % p, "dcu%d" % p, "dwu%d" % p, "dwl%d" % p, "cutv%d" % p
        Gn1, Gu1, vl = "Gn%d" % q, "Gu%d" % q, "vl%d" % q
        z0, z1 = 256 * t, 256 * t + 256
        v(dg(256), lambda: V.tensor_copy(T[Kn][:], T.CAN[:, 0:1024].indirect(T[vl][:])), ["CAN", vl], [Kn])
        v(dh(256), lambda: ts(T[Ku][:], T[Kn][:], -1.0, 2048.0, A.mult, A.add), [Kn], [Ku])
        for c in range(4):
            s(sg(1024), lambda c=c: S.activation(T[xg][:, 1024 * c:1024 * c + 1024],
              T.X[:, 0:4096].indirect(T[Gu][:, 64 * c:64 * c + 64]), AF.Copy), XC + [Gu], ["%s_%d" % (xg, c)])
        v(dh(256), lambda: ts(T.UW[:], T[Gn][:], T.RM1[:, k0:k0 + 1], T.RM2[:, k0:k0 + 1], A.mult, A.add), [Gn, "RM1", "RM2"], ["UW"])

        def callsL(B):
            r = []
            for h in range(2):
                r.append(lambda h=h: mm(B[:, 8 * h:8 * h + 8], T[Gn][:, 128 * h:128 * h + 128], T.selk[:, 8 * t:8 * t + 8], True, True))
                r.append(lambda h=h: mm(B[:, 16 + 8 * h:24 + 8 * h], T.UW[:, 128 * h:128 * h + 128], T.blk1[:], True, True))
            return r
        op("t", pe(64, 64, 64, 64), callsL, [Gn, "UW", "selk", "blk1"], [], tile="LwU%d" % t)
        op("s", sa(32), lambda B: [lambda: S.activation(T.LwU[:], B[:, 0:32], AF.Copy)], [], ["LwU"], tile="LwU%d" % t)
        tn = same(t, "w", "UW", 16, "LwU", "eqw", True)
        vp(one, lambda B: ts(T.nw[:], B[:, 0:16], T.thr[:], -10000.0, A.is_gt, A.mult), tn, ["thr"], ["nw"])
        v(one, lambda: V.tensor_tensor(T.n1w[:], T.nw[:], T.LwU[:, 0:16], A.add), ["nw", "LwU"], ["n1w"])
        v(dg(256), lambda: V.tensor_tensor(T.A2w[:], T.n1w[:, 0:16].indirect(T.zl[:, 0:16]), T.in1c[:], A.max), ["n1w", "zl", "in1c"], ["A2w"])
        spread_lists("A2w", "W2w%d" % t)
        vp(one, lambda B: ts(T[dwu][:], B[:, 0:16], -1.0, 63488.0, A.mult, A.add), "W2w%d" % t, [], [dwu])
        vp(one, lambda B: ts(T.ufw[:], B[:, 0:16], -0.25, 16896.625, A.mult, A.add), "W2w%d" % t, [], ["ufw"])
        v(one, lambda: ts(T[dwl][:], T.ufw[:], -1025.0, None, A.add), ["ufw"], [dwl])
        s(sg(256), lambda: S.activation(T.xw[:], T.X[:].indirect(T[dwu][:]), AF.Copy), XR + [dwu], ["xw"])
        s(sg(256), lambda: S.activation(T.cw[:], T.CAN[:].indirect(T[dwl][:]), AF.Copy), ["CAN", "CANd", dwl], ["cw"])
        v(dh(256), lambda: ts(T.r2[:], T.xw[:], 4.0, BIAS + 63.0, A.add, A.min), ["xw"], ["r2"])
        for h in range(2):
            s(sg(2048), lambda h=h: S.activation(T.zrep[:, 2048 * h:2048 * h + 2048], T.Z[:, z0:z1].indirect(T.zl[:, 128 * h:128 * h + 128]), AF.Copy),
              [Z, "zl"], ["zrep%d" % h])
        for h in range(2):
            v(dg(2048), lambda h=h: V.tensor_tensor(T.sc[:, 2048 * h:2048 * h + 2048], T.X[:, 0:4096].indirect(T[Ku][:, 128 * h:128 * h + 128]),
              T.zrep[:, 2048 * h:2048 * h + 2048], A.max), XC + [Ku, "zrep%d" % h], ["sc%d" % h])

            def callsK(B, h=h):
                r = [lambda: mm(B[:, 128 * h:128 * h + 128], T[Kn][:, 128 * h:128 * h + 128], T.I16[:], True, False)]
                for k in range(16):
                    r.append(lambda k=k: mm(B[:, 128 * h + k:128 * h + 128:16], T.sc[:, 2048 * h + k:2048 * h + 2048:16], T.blkS[:], False, k == 15))
                return r
            op("t", pe(128, *([64] * 16)), callsK, [Kn, "I16", "blkS", "sc%d" % h], [], tile="key%d" % t)
        vp(dv(256), lambda B: V.tensor_tensor_scan(T.sco[:], T.resetv[:], B[:, 0:256], 0.0, A.add, A.max), "key%d" % t, ["resetv"], ["sco"])
        v(one, lambda: ts(T.q1[:], T.sco[:, 15:256:16], 2047.0, None, A.add), ["sco"], ["q1"])
        v(one, lambda: ts(T.q2[:], T.q1[:], 4095, None, A.bitwise_and), ["q1"], ["q2"])
        v(one, lambda: ts(T[Lc][:], T.q2[:], -2047.0, None, A.add), ["q2"], [Lc])
        place(t, p, False)
        if not last:
            snt, arr = "snt%d" % (t + 1), "arr%d" % (t + 1)
            v(dg(256), lambda: V.tensor_tensor(T.xs[:], T.X[:, 0:4096].indirect(T[cu][:]), T.Z[:, z0:z1], A.add), XC + [cu, Z], ["xs"])
            v(dh(256), lambda: ts(T.ZS[:, z0:z1], T.xs[:], 0.5, -0.25, A.mult, A.add), ["xs"], ["zs%d" % t])
            dst = T.cores[(rank + 1 + t % 3) % len(T.cores)]
            rid, pid = topo.addr(dst)[0], topo.addr(dst)[1]
            ne = len(topo.engines(core, dst))
            op("g", 1.0, [lambda: g.remote_dma(T.Z[:, z1:z1 + 256], T.ZS[:, z0:z1], T.sem[arr], T.sem[snt], pid=pid, routing_id=rid,
                                               dma_engine_mask=topo.mask(core, dst))], ["zs%d" % t], ["way%d" % t], sem=snt, cnt=ne)
            op("x", 0.0, [], ["way%d" % t], ["Z%d" % (t + 1)], lat=2.5, sem=arr, cnt=ne)
        s(sg(256), lambda: S.activation(T[cutv][:], T.X[:, 0:4096].indirect(T[cu][:]), AF.Identity, bias=BIAS / 2 - 0.25, scale=0.5), XC + [cu], [cutv])
        op("t", pe(128, 128), lambda B: [lambda h=h: mm(B[:, 128 * h:128 * h + 128], T.A1[:, 128 * h:128 * h + 128], T.I16[:], True, True)
                                         for h in range(2)], ["A1", "I16"], [], tile="SP%d" % t)
        vp(dv(256), lambda B: V.tensor_copy(T.SPs[:], B[:, 0:256]), "SP%d" % t, [], ["SPs"])
        tn = same(t, "c", "SPs", 0, Lc, "eqc", False)
        vp(one, lambda B: ts(T.nc[:], B[:, 0:16], T.thr[:], -10000.0, A.is_gt, A.mult), tn, ["thr"], ["nc"])
        v(one, lambda: V.tensor_tensor(T.n1c[:], T.nc[:], T[Lc][:], A.add), ["nc", Lc], ["n1c"])
        v(dg(256), lambda: V.tensor_tensor(T.A2c[:], T.n1c[:, 0:16].indirect(T.zl[:, 0:16]), T.in1c[:], A.max), ["n1c", "zl", "in1c"], ["A2c"])
        spread_lists("A2c", "W2c%d" % t)
        vp(one, lambda B: ts(T[dcu][:], B[:, 0:16], -1.0, 63488.0, A.mult, A.add), "W2c%d" % t, [], [dcu])
        for b in range(8):
            tn = "d%d_%d" % (t, b)
            h, kb = b // 4, 4 * (b % 4)

            def callsD(B, h=h, kb=kb):
                r = []
                for j in range(4):
                    r.append(lambda j=j: mm(B[:, 128 * j:128 * j + 128], T.Ib[:], T[xg][:, 2048 * h + kb + j:2048 * h + 2048:16], True, False))
                    r.append(lambda j=j: mm(B[:, 128 * j:128 * j + 128], T.Ibn[:], T.Z[:, z0 + 128 * h:z0 + 128 * h + 128], False, True))
                return r
            op("t", pe(*([128] * 8)), callsD, ["Ib", "Ibn", Z] + ["%s_%d" % (xg, c) for c in (2 * h, 2 * h + 1)], [], tile=tn)
            op("s", sa(512), lambda B, b=b: [lambda: S.activation(T.ab[:, 512 * b:512 * b + 512], B[:], AF.Abs)], [], ["ab%d" % b], tile=tn)
            if b % 2 == 1:
                c = b // 2
                v(dh(1024), lambda c=c: ts(T.th[:, 1024 * c:1024 * c + 1024], T.ab[:, 1024 * c:1024 * c + 1024], T.lim[:, t:t + 1], None, A.is_gt),
                  ["ab%d" % (b - 1), "ab%d" % b, "lim%d" % t], ["th%d" % c])
        for c in range(4):
            h = c // 2
            op("t", pe(*([64] * 8)), lambda B, c=c, h=h: [
                lambda k=k: mm(B[:, 128 * h + k:128 * h + 128:16], T.th[:, 2048 * h + 128 * k:2048 * h + 128 * k + 128], T.blkb[:], True, True)
                for k in range(8 * (c % 2), 8 * (c % 2) + 8)], ["th%d" % c, "blkb"], [], tile="cnt%d" % t)
        vp(dv(256), lambda B: ts(T.sevL[:], B[:, 0:256], 8.5, None, A.is_gt), "cnt%d" % t, [], ["sevL"])
        vp(dv(256), lambda B: V.tensor_tensor(T.sevT[:], B[:, 0:256], T.thrk[:, 15 - t:271 - t], A.is_gt), "cnt%d" % t, ["thrk"], ["sevT"])
        s(sg(256), lambda: S.activation(T.skrep[:], T.sevL[:].indirect(T.skl[:, 16 * t:16 * t + 16]), AF.Copy), ["sevL", "skl"], ["skrep"])
        if not last:
            op("t", pe(64), lambda B: [lambda: mm(B[:, 0:16], T.onesb[:], T.sevL[:, k0:256:16], True, True)], ["onesb", "sevL"], [], tile="S%d" % t)
            op("s", sa(16) + 0.14, lambda B: [lambda: S.activation(T.sj[:], B[:, 0:16], AF.Identity, bias=385.0, accum_out=T.sf[:])],
               [], ["sf"], tile="S%d" % t)
            v(one, lambda: ts(T.si[:], T.sf[:], 0.25, -4.375, A.mult, A.add), ["sf"], ["si"])
            v(one, lambda: ts(T.lim[:, t + 1:t + 2], T.si[:], -4.0, T.sf[:], A.mult, A.add), ["si", "sf"], ["lim%d" % (t + 1)])

        def blend(ident, extra, sevs):
            def calls(B):
                r = []
                for o, m in ((0, "I8n"), (256, "I8p")):
                    r.append(lambda o=o: mm(B[:, o:o + 256], ident, T[Gn][:], True, False))
                    if extra:
                        r.append(lambda o=o: mm(B[:, o:o + 256], T.wide[:, 15 - t:143 - t], T.SPs[:], False, False))
                    for n in sevs:
                        for h in range(2):
                            r.append(lambda o=o, m=m, h=h, n=n: mm(B[:, o + 128 * h:o + 128 * h + 128], T[n][:, 128 * h:128 * h + 128], T[m][:],
                                                                   False, h == 1 and n == sevs[-1]))
                return r
            return calls
        op("t", pe(*([256] * 6)), blend(T.It[:, 128 * t:128 * t + 128], True, ["sevT"]),
           ["It", Gn, "wide", "SPs", "sevT", "I8n", "I8p"], [], tile="G%d" % t)
        vp(dv(256), lambda B: V.tensor_tensor(T.gm[:], T[Kn][:], B[:, 0:256], A.max), "G%d" % t, [Kn], ["gm"])
        vp(dv(256), lambda B: V.tensor_tensor(T[Gn1][:], T.gm[:], B[:, 256:512], A.min), "G%d" % t, ["gm"], [Gn1])
        if not last:
            v(dh(256), lambda: ts(T[Gu1][:], T[Gn1][:], -1.0, 2048.0, A.mult, A.add), [Gn1], [Gu1])
        op("t", pe(*([256] * 6)), blend(T.I16[:], False, ["sevL", "skrep"]), ["I16", Gn, "sevL", "skrep", "I8n", "I8p"], [], tile="N%d" % t)
        vp(dv(256), lambda B: V.tensor_tensor(T.cm[:], T.cw[:], B[:, 0:256], A.max), "N%d" % t, ["cw"], ["cm"])
        vp(dv(256), lambda B: V.tensor_tensor(T.cn[:], T.cm[:], B[:, 256:512], A.min), "N%d" % t, ["cm"], ["cn"])
        v(ds(256), lambda: V.tensor_copy(T.CAN[:].indirect(T[dwl][:]), T.cn[:]), ["cn", dwl], ["CAN", "CANd"])

        def callsR(B):
            r = [lambda: mm(B[:, 0:256], T.Ih[:], T.xw[:], True, False),
                 lambda: mm(B[:, 0:256], T.Ih[:], T.Z[:, z0:z1], False, False),
                 lambda: mm(B[:, 0:256], T.qtr[:], T.ones16[:], False, False)]
            for h in range(2):
                r.append(lambda h=h: mm(B[:, 128 * h:128 * h + 128], T.skrep[:, 128 * h:128 * h + 128], T.I5n[:], False, h == 1))
            for h in range(2):
                r.append(lambda h=h: mm(B[:, 256 + 128 * h:384 + 128 * h], T.skrep[:, 128 * h:128 * h + 128], T.Ib[:], True, True))
            return r
        op("t", pe(256, 256, 256, 128, 128, 128, 128), callsR, ["Ih", "xw", Z, "qtr", "ones16", "skrep", "I5n", "Ib"], [], tile="R%d" % t)
        vp(dv(256), lambda B: V.tensor_tensor(T.r2m[:], T.r2[:], B[:, 256:512], A.mult), "R%d" % t, ["r2"], ["r2m"])
        vp(dv(256), lambda B: V.tensor_tensor(T.rn[:], T.r2m[:], B[:, 0:256], A.max), "R%d" % t, ["r2m"], ["rn"])
        v(ds(256), lambda: V.tensor_copy(T.X[:].indirect(T[dwu][:]), T.rn[:]), ["rn", dwu], XR)
        v(ds(256), lambda: V.tensor_copy(T.X[:].indirect(T[dcu][:]), T[cutv][:]), [cutv, dcu], XR)

    for t in range(NT):
        step(t)

    def store(name, out, src, R):
        op("y", 0.1, [lambda: Y.dma_start(out, src)], R, ["y" + name], lat=3.0, sem="st_" + name, cnt=16)

    s(sa(1024), lambda: S.activation(T.lo[:], T.CAN[:, 0:1024], AF.Identity, bias=2048.0, scale=-1.0), ["CAN"], ["lo"])
    store("ol", T.yl[:], T.lo[:], ["lo"])
    v(dv(256), lambda: ts(T.go[:], T["Gn%d" % (NT % 2)][:], -1.0, 2048.0, A.mult, A.add), ["Gn%d" % (NT % 2)], ["go"])
    store("og", T.yg[:], T.go[:], ["go"])
    for c in range(4):
        a, b = 1024 * c, 1024 * c + 1024
        if c < 3:
            v(dh(1024), lambda a=a, b=b: ts(T.th[:, a:b], T.X[:, a:b], -BIAS, None, A.add), ["X%d" % c], ["th%d" % c])
        else:
            s(sa(1024), lambda a=a, b=b: S.activation(T.th[:, a:b], T.X[:, a:b], AF.Identity, bias=-BIAS), ["X%d" % c], ["th%d" % c])
        store("o%d" % c, T.yx[:, a:b], T.th[:, a:b], ["th%d" % c])
    emit(g, T, ops, schedule(ops))


def depend(ops):
    last, readers, tiles = {}, {}, {}
    for o in ops:
        d = set()
        for r in o["R"]:
            d.update(last.get(r, ()))
        for w in o["W"]:
            d.update(last.get(w, ()))
            d.update(readers.get(w, ()))
        for r in o["R"]:
            readers.setdefault(r, []).append(o["i"])
        for w in o["W"]:
            last[w] = [o["i"]]
            readers[w] = []
        if o["tile"]:
            tl = tiles.setdefault(o["tile"], [None, [], []])
            if tl[0] != o["e"]:
                tl[0], tl[1], tl[2] = o["e"], tl[2], []
            d.update(tl[1])
            tl[2].append(o["i"])
        d.discard(o["i"])
        o["d"] = d


def schedule(ops):
    depend(ops)
    n = len(ops)
    succ = [[] for _ in range(n)]
    for o in ops:
        for j in o["d"]:
            succ[j].append(o["i"])
    prio = [0.0] * n
    for i in range(n - 1, -1, -1):
        prio[i] = ops[i]["c"] + ops[i]["lat"] + SYNC + max([prio[j] for j in succ[i]] or [0.0])
    for o in ops:
        prio[o["i"]] += BONUS.get("".join(c for c in (o["W"] or [o["tile"]])[0] if c.isalpha()) + "_" + o["e"], 0.0)
    users = {}
    for o in ops:
        if o["tile"]:
            users.setdefault(o["tile"], []).append(o["i"])
    left = {k: len(u) for k, u in users.items()}
    bank = {}
    free = {k: [] for k in range(8)}
    need = [len(o["d"]) for o in ops]
    rt, fin = [0.0] * n, [0.0] * n
    ready = [i for i in range(n) if need[i] == 0]
    et = {"v": 0.0, "s": 0.0, "t": 0.0, "g": 0.0, "y": 0.0, "x": 0.0}
    order = []
    while ready:
        cand = []
        for i in ready:
            o = ops[i]
            st = max(rt[i], et[o["e"]] if o["e"] != "x" else 0.0)
            bk = None
            if o["tile"] and o["tile"] not in bank:
                if not free:
                    continue
                a, bk = min((max([fin[u] for u in us] or [0.0]), k) for k, us in free.items())
                st = max(st, a + SYNC)
            cand.append((st, -prio[i], i, bk))
        if not cand:
            raise ValueError("no bank for any ready op")
        st, _, i, bk = min(cand, key=lambda c: c[:3])
        ready.remove(i)
        o = ops[i]
        if bk is not None:
            bank[o["tile"]] = bk
            o["d"] = set(o["d"]) | set(free.pop(bk))
        if o["tile"]:
            o["b"] = bank[o["tile"]]
            left[o["tile"]] -= 1
            if left[o["tile"]] == 0:
                free[o["b"]] = users[o["tile"]]
        et[o["e"]] = st + o["c"]
        fin[i] = st + o["c"] + o["lat"]
        o["t0"] = st
        order.append(i)
        for j in succ[i]:
            need[j] -= 1
            rt[j] = max(rt[j], fin[i] + SYNC)
            if need[j] == 0:
                ready.append(j)
    if len(order) != n:
        raise ValueError("schedule stuck")
    return order


def emit(g, T, ops, order):
    Q = {"v": g.vector, "s": g.scalar, "t": g.tensor, "g": g, "y": g.sync}
    known = {e: {} for e in Q}
    count, done = {}, {}
    for i in order:
        o = ops[i]
        e = o["e"]
        if e == "x":
            done[i] = (o["sem"], o["cnt"], {})
            continue
        kn = known[e]
        for _, j in sorted(((ops[j]["t0"], j) for j in o["d"]), reverse=True):
            sm, c, snap = done[j]
            if c > kn.get(sm, 0):
                Q[e].wait_ge(T.sem[sm], c)
                kn[sm] = c
                for a, b in snap.items():
                    if b > kn.get(a, 0):
                        kn[a] = b
        calls = o["f"](T["ps%d" % o["b"]]) if o["tile"] else o["f"]
        for f in calls:
            r = f()
            if o["sem"] is None:
                count["q" + e] = count.get("q" + e, 0) + 1
                r.then_inc(T.sem["q" + e], 1)
            elif not o["sem"].startswith("snt"):
                r.then_inc(T.sem[o["sem"]], 16)
        done[i] = (o["sem"] or "q" + e, o["cnt"] or count.get("q" + e, 0), dict(kn))
    for sm in sorted(count):
        g.wait_ge(T.sem[sm], count[sm])
    for o in ops:
        if o["sem"] is not None:
            g.wait_ge(T.sem[o["sem"]], o["cnt"])
